import numpy as np, ml_dtypes
CORES = [16,18,20,22]
N = 4
import mx_ref
BF = ml_dtypes.bfloat16
def gentries(a):
    return np.ascontiguousarray(a.reshape(8, 16, -1).transpose(0, 2, 1)).reshape(8, -1)
def gtable(e):
    e = np.asarray(e); return np.ascontiguousarray(e.reshape(8, -1, 16).transpose(0, 2, 1)).reshape(128, -1).astype(np.int32)
def gcols(t, e):
    v = np.concatenate([t.reshape(8, 16, -1, 4), np.zeros((8, 16, 1, 4), BF)], axis=2)
    return np.ascontiguousarray(np.stack([v[g][:, e[g]] for g in range(8)])).reshape(128, -1)
def tile(rs):
    return np.stack(rs, axis=2).reshape(128, -1).astype(BF)
def pick(q, e):
    c = np.concatenate([q[0].reshape(128, -1, 4), np.zeros((128, 1, 4), np.uint8)], axis=1); s = np.concatenate([q[1], np.ones((16, 1), np.uint8)], axis=1)
    return (np.ascontiguousarray(c[:, e].reshape(128, -1)), np.ascontiguousarray(s[:, e]))
def join(*qs):
    return (np.concatenate([q[0] for q in qs], axis=1), np.concatenate([q[1] for q in qs], axis=1))
def put(q, e, v):
    c, s = q[0].reshape(128, -1, 4).copy(), q[1].copy(); c[:, e] = v[0].reshape(128, -1, 4); s[:, e] = v[1]
    return (c.reshape(128, -1), s)
def pk(c, s):
    return (np.ascontiguousarray(c), mx_ref.live(s))
def emit(q):
    return q[0], q[1]
def packed(v, rng):
    q = [mx_ref.quantize(np.ascontiguousarray(v[r])) for r in range(N)]
    return np.stack([a for a, b in q]), np.stack([mx_ref.plane(b, rng) for a, b in q])
def values_of_codes():
    e, c = np.zeros((128, 128, 4), np.float32), np.zeros((128, 2, 4), np.uint8)
    e[np.arange(128), np.arange(128), 0] = 1
    c[:127, :, 0] = np.arange(256).reshape(2, 128).T[:127]
    return mx_ref.matmul(mx_ref.quantize(e.reshape(128, 512).astype(BF)), (c.reshape(128, 8), np.full((16, 2), 127, np.uint8))).T.reshape(-1).astype(np.float64)
CODE_VALUE, SCALE_VALUE = values_of_codes(), 2.0 ** (np.arange(256) - 127.0)
def decode(q):
    return (CODE_VALUE[q[0]].reshape(16, 8, -1, 4) * SCALE_VALUE[q[1]][:, None, :, None] + 0.0).reshape(128, -1).astype(np.float32)
def f(rng, *shape):
    return mx_ref.flush((rng.standard_normal(shape, dtype=np.float32) * np.exp2(rng.integers(-2, 3, shape[:-1] + (1,)))).astype(BF))
def wide(rng, *shape, cols=0):
    v = rng.standard_normal(shape, dtype=np.float32) * np.exp2(rng.integers(-12, 13, shape)).astype(np.float32)
    if cols: v *= np.repeat(np.exp2(rng.integers(-cols, cols + 1, shape[:-2] + (1, shape[-1] // 4))) * (rng.random(shape[:-2] + (1, shape[-1] // 4)) > 0.0625), 4, axis=-1).astype(np.float32)
    return mx_ref.flush(v.astype(BF))
C, T, R = 320, 128, 3
STEP = [1, 2, 1]
def big(v):
    v = v.astype(np.float32)
    v[np.abs(v) < np.float32(2.0 ** -16)] = 0
    return v.astype(BF)
def numbers_of(rng):
    return {"x": big(f(rng, N, 128, 4 * C)), "bm": big(f(rng, N, 128, 4 * C)), "u": np.array(f(rng, N, 128, 512)), "v": np.array(f(rng, N, 128, 512))}
def stored(a):
    return {"co": np.stack([gtable(e) for e in a]), "cn": np.stack([gtable(np.concatenate([a[(r + s) % N][:, :T] for s in STEP], axis=1)) for r in range(N)])}
def anywhere(rng):
    return rng.integers(0, C, (N, 8, C))
def weights(rng, w):
    c, p = packed(w, rng)
    return {"wc": c, "ws": p}
def straight(rng, size):
    w = np.zeros((N, 128, 4, 128, 4), np.float32)
    i = np.arange(128)
    for k in range(4): w[:, i, k, i, k] = np.tile(size, 8)
    return weights(rng, w.reshape(N, 128, 2048).astype(BF))
def signs(rng):
    return np.stack([rng.permutation(8) % 2 * 2.0 - 1.0 for r in range(N)])
def setup_inputs(rng):
    return {**numbers_of(rng), **stored(anywhere(rng)), **weights(rng, f(rng, N, 128, 2048))}
def setup_inputs_ties(rng):
    d = numbers_of(rng)
    e = rng.permutation(N)
    x = d["x"].reshape(N, 8, 16, C, 4)
    bm = d["bm"].reshape(N, 8, 16, C, 4)
    for r in range(N):
        k = np.zeros(C, int) if r == e[0] else rng.permutation(C) % 3
        a = x[r][:, :8, :3].copy()
        a[:, :, 2] = 0
        x[r][:, :8] = a[:, :, k]
        bm[r][:, :8] = bm[r][:, :8, :1].copy()
        bm[r][rng.permutation(8) < 3, :8] = 0
    x[e[1]] = 0
    u = d["u"].reshape(N, 8, 16, 128, 4)
    u[:, :, 8:, ::16] = 0
    for g in range(8):
        for h in range(8):
            if h != g: u[:, h, :, 16 * g] = 0
    w = np.array(f(rng, N, 128, 2048)).reshape(N, 8, 16, 4, 8, 16, 4)
    w[:, :, :, :, :, :8] = 0
    return {"x": x.reshape(N, 128, 4 * C), "bm": bm.reshape(N, 128, 4 * C), "u": u.reshape(N, 128, 512), "v": d["v"], **stored(anywhere(rng)), **weights(rng, w.reshape(N, 128, 2048))}
def setup_inputs_near(rng):
    d = numbers_of(rng)
    o = rng.permutation(N)
    x = d["x"].astype(np.float32).reshape(N, 8, 16, C, 4)
    bm = d["bm"].astype(np.float32).reshape(N, 8, 16, C, 4)
    u = d["u"].astype(np.float32).reshape(N, 128, 128, 4)
    u[:, :, ::16] = 0
    for z in (x, bm):
        z[:, :, 11:] = rng.integers(4, 8, (N, 8, 5, C, 4)) * rng.choice([-1.0, 1.0], (N, 8, 5, C, 4)) * 2.0 ** -20
        for i in (0, 8, 9, 10): z[:, :, i] = 0
    sg = signs(rng)
    for r in range(N):
        small = o[r] % 2 == 1
        e = 2.0 ** -30 if small else 2.0 ** -23
        k = 1.0 if o[r] % 4 == 0 else 2.0 ** -30
        s = np.arange(C) // 2 if o[r] // 2 % 2 == 0 else np.arange(C) % (C // 2) // 2
        digit = (s[:, None] >> np.arange(8)) & 1
        turn = rng.choice([-1.0, 1.0])
        for g in range(8):
            a = (digit - 1 if small and sg[r, g] < 0 else digit) * e * np.exp2(np.arange(8))
            x[r, g, 8] = a[:, :4]
            x[r, g, 9] = a[:, 4:]
            if not small: x[r, g, 0, :, 0] = sg[r, g]
            if g % 2:
                j = int(rng.integers(C // 4))
                x[r, g, 0, j, 0] = -2.0 ** 30
                x[r, g, 0, j + C // 2, 0] = -2.0 ** 30
            one = rng.choice([-1.0, 1.0])
            bm[r, g, 10, 0, 0] = one * (8 if small and g < 4 else 512) * e
            h = 16 * g
            u[r, h, h, 0] = k
            u[r, h + 8:h + 10, h] = k
            u[r, h + 10, h, 0] = one * (turn if g % 2 else -turn) * k
            if small and g < 2:
                bm[r, g, 10, 0, 1] = bm[r, g, 10, 0, 0]
                u[r, h + 10, h, 1] = -u[r, h + 10, h, 0]
                u[r, h + 10, h, 0] *= 1.125
    size = np.full(16, 32.0)
    size[[0, 8, 9, 10]] = 0
    return {"x": x.reshape(N, 128, 4 * C).astype(BF), "bm": bm.reshape(N, 128, 4 * C).astype(BF), "u": u.reshape(N, 128, 512).astype(BF), "v": d["v"], **stored(anywhere(rng)), **straight(rng, size)}
def setup_inputs_huge(rng):
    d = numbers_of(rng)
    o = rng.permutation(N)
    x = 2.0 ** 30 * (0.5 + 0.1 * rng.random((N, 128, C, 4)))
    c = np.stack([rng.permutation(C) % 2 * 2.0 - 1.0 for r in range(N)])
    c[o < N // 2] = 1
    x *= c[:, None, :, None]
    bm = 2.0 ** 27 * (0.5 + 0.5 * rng.random((N, 128, 4 * C))) * (o % 2 * 2.0 - 1.0)[:, None, None]
    u = d["u"].reshape(N, 128, 128, 4)
    a = 2.0 ** 30 * (1 - 0.25 * rng.random((N, 128, 8, 4))) * signs(rng)[:, None, :, None]
    u[:, :, ::16] = a.astype(np.float32).astype(BF)
    return {"x": x.astype(np.float32).reshape(N, 128, 4 * C).astype(BF), "bm": bm.astype(np.float32).astype(BF), "u": u.reshape(N, 128, 512), "v": d["v"], **stored(anywhere(rng)), **straight(rng, np.full(16, 4.0))}
def setup_inputs_coords(rng):
    a = anywhere(rng)
    i = np.arange(C)
    for r in range(N):
        g = rng.permutation(8)
        a[r, g[0]] = int(rng.integers(C))
        a[r, g[1]] = rng.permutation(C) % 2 * (C - 1)
        a[r, g[2]] = i
        a[r, g[3]] = C - 1 - i
        a[r, g[4]] = i % 2
    return {**numbers_of(rng), **stored(a), **weights(rng, f(rng, N, 128, 2048))}
def setup_inputs_spread(rng):
    d = setup_inputs(rng)
    d["x"] = big(wide(rng, N, 128, 4 * C, cols=6))
    d["bm"] = big(wide(rng, N, 128, 4 * C, cols=6))
    return d
def check_inputs(d):
    b = []
    for k in ("x", "bm", "u", "v"):
        a = np.abs(d[k].astype(np.float32))
        if not (np.isfinite(a).all() and ((a == 0) | (a >= 2.0 ** -30) & (a <= 2.0 ** 30)).all()): b.append("a value of " + k)
    for k in ("co", "cn"):
        if ((d[k] < 0) | (d[k] >= C)).any(): b.append("an entry of " + k)
    for r in range(N):
        e = np.concatenate([gentries(d["co"][(r + s) % N])[:, :T] for s in STEP], axis=1)
        if (gentries(d["cn"][r]) != e).any(): b.append("cn isn't what co of other ranks says")
    if (d["wc"] % 128 == 127).any(): b.append("a code of wc that is no number")
    for p in d["ws"]:
        s = mx_ref.live(p)
        if ((s < 1) | (s > 157)).any(): b.append("a scale of ws")
    return b
def reference(x, bm, u, v, co, cn, wc, ws):
    qu = [mx_ref.quantize(u[r]) for r in range(N)]
    lay = [pk(wc[r], ws[r]) for r in range(N)]
    now, beam = [x[r] for r in range(N)], [bm[r] for r in range(N)]
    half = C // 2
    ol = np.zeros((N, 8, 2 * R), np.float32)
    for t in range(R):
        left, sent = [], []
        for r in range(N):
            p = mx_ref.matmul(qu[r], mx_ref.quantize(now[r]))[::16] + np.float32(0.0)
            s = mx_ref.matmul(qu[r], mx_ref.quantize(np.ascontiguousarray(beam[r][:, :16])))[::16, 0]
            k = np.argmax(p.reshape(8, 2, half), axis=2) + np.array([0, half])
            best = np.take_along_axis(p, k, axis=1)
            h = np.where(best[:, 1] > best[:, 0], k[:, 1], k[:, 0])
            c = np.repeat(np.where(s > 0, np.float32(0.5), np.float32(-0.5)), 16)[:, None]
            own = gentries(co[r])
            far = gentries(cn[r])[:, T * t:T * t + T]
            e = np.abs(own - np.repeat(np.take_along_axis(own, k, axis=1), half, axis=1))
            left.append(now[r].astype(np.float32) - c * gcols(beam[r], e).astype(np.float32))
            e = np.abs(far - np.take_along_axis(own, h[:, None], axis=1))
            sent.append(mx_ref.quantize((c * gcols(beam[r], e).astype(np.float32)).astype(BF)))
            ol[r, :, 2 * t:2 * t + 2] = k
        for r in range(N):
            left[r][:, :4 * T] = left[r][:, :4 * T] - decode(sent[(r - STEP[t]) % N])
            now[r] = left[r].astype(BF)
            if t < R - 1:
                q = mx_ref.quantize(now[r])
                beam[r] = tile([mx_ref.matmul(pick(lay[r], np.arange(128 * b, 128 * b + 128)), q) * np.float32(0.015625) + beam[r][:, b::4].astype(np.float32) * np.float32(0.5) for b in range(4)])
    y = np.zeros((N, 128, C), np.float32)
    oc, osc = np.zeros((N, 128, 4 * C), np.uint8), np.zeros((N, 16, C), np.uint8)
    for r in range(N):
        q = mx_ref.quantize(now[r])
        y[r] = mx_ref.matmul(mx_ref.quantize(v[r]), q)
        oc[r], osc[r] = emit(q)
    return {"y": y, "ol": ol, "oc": oc, "osc": osc}

@@ -1,0 +1,463 @@
+from concourse.mybir import dt, AluOpType, ActivationFunctionType
+
+ALU = AluOpType
+ACT = ActivationFunctionType
+C, TL, ROUNDS = 320, 128, 3
+HALF = C // 2
+STEP = [1, 2, 1]
+LOW = -9.0e29
+CODES, PLANE = "float8_e4m3fn_x4", "uint8"
+
+SCRATCH = {
+    "bms": ("sbuf", [128, 4 * C], "bfloat16"),
+    "us": ("sbuf", [128, 512], "bfloat16"),
+    "vs": ("sbuf", [128, 512], "bfloat16"),
+    "qu": ("sbuf", [128, 128], CODES), "su": ("sbuf", [128, 128], PLANE),
+    "qur": ("sbuf", [128, 128], CODES), "sur": ("sbuf", [128, 128], PLANE),
+    "qv": ("sbuf", [128, 128], CODES), "sv": ("sbuf", [128, 128], PLANE),
+    "wq": ("sbuf", [128, 512], CODES), "wsc": ("sbuf", [128, 512], PLANE),
+    "qe": ("sbuf", [128, 512], CODES), "se": ("sbuf", [128, 512], PLANE),
+    "cc": ("sbuf", [128, 44], "int32"), "ccf": ("sbuf", [128, 44], "float32"),
+    "co16": ("sbuf", [128, 20], "uint16"),
+    "uo32": ("sbuf", [128, 8], "int32"), "uo16": ("sbuf", [128, 8], "uint16"),
+    "jp": ("sbuf", [128, 128], "bfloat16"), "band": ("sbuf", [128, 520], "bfloat16"),
+    "ramp": ("sbuf", [128, C], "float32"), "coord": ("sbuf", [128, C], "float32"),
+    "neg": ("sbuf", [128, HALF], "float32"),
+    "z": ("sbuf", [128, 512], "bfloat16"),
+    "hcol": ("sbuf", [128, 8], "float32"),
+    "junk": ("sbuf", [128, C], "float32"),
+    "ysb": ("sbuf", [128, C], "float32"),
+    "ps": ("psum", [128, 4096], "float32"),
+}
+for _t in range(ROUNDS + 1):
+    SCRATCH["xs%d" % _t] = ("sbuf", [128, 4 * C], "bfloat16")
+    SCRATCH["qx%d" % _t] = ("sbuf", [128, C], CODES)
+    SCRATCH["sx%d" % _t] = ("sbuf", [128, C], PLANE)
+for _t in range(ROUNDS):
+    SCRATCH["run%d" % _t] = ("sbuf", [128, C], "float32")
+    SCRATCH["yk%d" % _t] = ("sbuf", [128, 4], "float32")
+    SCRATCH["kk%d" % _t] = ("sbuf", [128, 4], "uint16")
+    SCRATCH["na%d" % _t] = ("sbuf", [128, 48], "float32")
+    SCRATCH["abt%d" % _t] = ("sbuf", [128, 8], "float32")
+    SCRATCH["abe%d" % _t] = ("sbuf", [128, 20], "float32")
+    SCRATCH["oft%d" % _t] = ("sbuf", [128, 32], "uint16")
+    SCRATCH["ofe%d" % _t] = ("sbuf", [128, 20], "uint16")
+    SCRATCH["cs%d" % _t] = ("sbuf", [128, 4], "float32")
+    SCRATCH["win%d" % _t] = ("sbuf", [128, 4 * C], "bfloat16")
+    SCRATCH["gt%d" % _t] = ("sbuf", [128, 4 * TL], "bfloat16")
+    SCRATCH["qg%d" % _t] = ("sbuf", [128, TL], CODES)
+    SCRATCH["sg%d" % _t] = ("sbuf", [128, TL], PLANE)
+    SCRATCH["lq%d" % _t] = ("sbuf", [128, TL], CODES)
+    SCRATCH["ls%d" % _t] = ("sbuf", [128, TL], PLANE)
+    SCRATCH["qz%d" % _t] = ("sbuf", [128, 128], CODES)
+    SCRATCH["sz%d" % _t] = ("sbuf", [128, 128], PLANE)
+    SCRATCH["el%d" % _t] = ("sbuf", [128, 4 * TL], "float32")
+for _t in range(ROUNDS - 1):
+    SCRATCH["aux%d" % _t] = ("sbuf", [128, 4 * C], "bfloat16")
+    SCRATCH["bp%d" % (_t + 1)] = ("sbuf", [128, 4 * C], "bfloat16")
+
+SEMAPHORES = ["cv", "cs", "cp", "cg", "lu", "lx0", "lx1", "lbm", "lz", "lcc", "lw", "lv",
+              "sty", "sts", "arr0", "arr1", "arr2", "loc"]
+COUNTER = {"V": "cv", "S": "cs", "P": "cp", "G": "cg"}
+
+
+def R(name, lo=0, hi=1 << 20, plane=None):
+    return (name, lo, hi, plane)
+
+
+def bank(k):
+    return ("ps", k, k + 1, None)
+
+
+def meets(a, b):
+    return a[0] == b[0] and a[1] < b[2] and b[1] < a[2] and (a[3] is None or b[3] is None or a[3] == b[3])
+
+
+def clash(a, b):
+    for w in a["w"]:
+        for r in b["r"] + b["w"]:
+            if meets(w, r):
+                return True
+    for r in a["r"]:
+        for w in b["w"]:
+            if meets(r, w):
+                return True
+        if r[0] == "ps" and a["q"] != b["q"]:
+            for r2 in b["r"]:
+                if meets(r, r2):
+                    return True
+    return False
+
+
+def emit(g, T, ops, ends):
+    queue = {"V": g.vector, "S": g.scalar, "P": g.tensor, "G": g, "Y": g.sync}
+    known = {q: {} for q in queue}
+    place = {q: 0 for q in queue}
+    total = {}
+    for n, op in enumerate(ops):
+        q = op["q"]
+        need = {}
+        for a in ops[:n]:
+            if clash(a, op):
+                key = a["key"]
+                if known[q].get(key, 0) < a["pos"] and (key not in need or need[key]["pos"] < a["pos"]):
+                    need[key] = a
+        waits = []
+        for a in sorted(need.values(), key=lambda e: -e["n"]):
+            if known[q].get(a["key"], 0) >= a["pos"]:
+                continue
+            waits.append(a)
+            a["mark"] = True
+            for k, v in a["seen"].items():
+                if known[q].get(k, 0) < v:
+                    known[q][k] = v
+            known[q][a["key"]] = total[a["key"]] if a["sem"] else a["pos"]
+        op["waits"] = [(a, total[a["key"]] if a["sem"] else None) for a in waits]
+        op["seen"] = dict(known[q])
+        op["n"] = n
+        if op["sem"]:
+            op["key"] = op["sem"]
+            total[op["key"]] = total.get(op["key"], 0) + 16
+            op["pos"] = total[op["key"]]
+        else:
+            op["key"] = q
+            place[q] += 1
+            op["pos"] = place[q]
+    count = {q: 0 for q in queue}
+    for op in ops:
+        if op.get("mark") and not op["sem"]:
+            count[op["q"]] += 1
+            op["count"] = count[op["q"]]
+    for op in ops:
+        e = queue[op["q"]]
+        for sem, val in op["ext"]:
+            e.wait_ge(T.sem[sem], val)
+        for a, val in op["waits"]:
+            if a["sem"]:
+                e.wait_ge(T.sem[a["sem"]], val)
+            else:
+                e.wait_ge(T.sem[COUNTER[a["q"]]], a["count"])
+        ins = op["f"]()
+        if op["sem"]:
+            ins.then_inc(T.sem[op["sem"]], 16)
+        elif op.get("mark"):
+            ins.then_inc(T.sem[COUNTER[op["q"]]], 1)
+    for q, sem, val in ends:
+        queue[q].wait_ge(T.sem[sem], total[sem] if val is None else val)
+
+
+def rank_program(g, core, T, topo):
+    rank = T.rank_of(core)
+    if rank is None:
+        return
+    n_ranks = len(T.cores)
+    V, S, P, Y = g.vector, g.scalar, g.tensor, g.sync
+    ops = []
+
+    def add(q, f, r, w, sem=None, ext=()):
+        ops.append({"q": q, "f": f, "r": list(r), "w": list(w), "sem": sem, "ext": list(ext)})
+
+    def quant(codes, scales, a, b, view, rd):
+        add("V", lambda: V.quantize_mx(T[codes][:, a:b], T[scales][:, a:b], view),
+            rd, [R(codes, a, b), R(scales, a, b)])
+
+    def mm(k, lq, ls, la, rq, rs, a, b, ext=()):
+        add("P", lambda: P.matmul_mx(T.ps[:, 512 * k:512 * k + b - a], T[lq][:, la:la + 128], T[ls][:, la:la + 128],
+                                     T[rq][:, a:b], T[rs][:, a:b], True, True),
+            [R(lq, la, la + 128), R(ls, la, la + 128), R(rq, a, b), R(rs, a, b)], [bank(k)], ext=ext)
+
+    def quant_x(t, a, b):
+        quant("qx%d" % t, "sx%d" % t, a, b, T["xs%d" % t][:, 4 * a:4 * b], [R("xs%d" % t, a, b)])
+
+    def scan(t, f, k):
+        run = T["run%d" % t]
+        add("V", lambda: V.tensor_tensor_scan(run[:, HALF * f:HALF * f + HALF], T.ps[:, 512 * k:512 * k + HALF],
+                                              T.neg[:], LOW, ALU.max, ALU.max),
+            [bank(k), R("neg")], [R("run%d" % t, HALF * f, HALF * f + HALF)])
+
+    def count(t, f):
+        run, yk = T["run%d" % t], T["yk%d" % t]
+        col = 1 if f == 0 else 3
+        a, b = HALF * f, HALF * f + HALF
+        add("S", lambda: S.activation(T.junk[:, a:b], run[:, a:b], ACT.Sign, bias=run[:, b - 1:b], scale=-1.0,
+                                      accum_out=yk[:, col:col + 1]),
+            [R("run%d" % t, a, b)], [R("junk", a, b), R("yk%d" % t, col, col + 1)])
+
+    def peak1(t, q):
+        yk = T["yk%d" % t]
+        if q == "V":
+            f = lambda: V.tensor_scalar(yk[:, 2:3], yk[:, 3:4], float(HALF), None, ALU.add)
+        else:
+            f = lambda: S.activation(yk[:, 2:3], yk[:, 3:4], ACT.Identity, bias=T.ramp[:, HALF:HALF + 1])
+        add(q, f, [R("yk%d" % t, 3, 4), R("ramp")], [R("yk%d" % t, 2, 3)])
+
+    def higher(t):
+        run, yk = T["run%d" % t], T["yk%d" % t]
+        add("V", lambda: V.tensor_scalar(yk[:, 0:1], run[:, HALF - 1:HALF], run[:, C - 1:C], yk[:, 2:3],
+                                         ALU.is_lt, ALU.mult),
+            [R("run%d" % t), R("yk%d" % t, 2, 3)], [R("yk%d" % t, 0, 1)])
+
+    def peaks16(t):
+        yk, kk = T["yk%d" % t], T["kk%d" % t]
+        add("V", lambda: V.tensor_scalar(kk[:, 0:3], yk[:, 0:3], yk[:, 1:2], None, ALU.max),
+            [R("yk%d" % t, 0, 3)], [R("kk%d" % t)])
+
+    def store_peaks(t):
+        yk = T["yk%d" % t]
+        add("Y", lambda: Y.dma_start(T.ol[:, 2 * t:2 * t + 2], yk[0:128:16, 1:3]), [R("yk%d" % t, 1, 3)], [], sem="sty")
+
+    def peak_coords(t):
+        add("S", lambda: S.activation(T["na%d" % t][:], T.coord[:].indirect(T["kk%d" % t][:, 0:3]), ACT.Copy, scale=-1.0),
+            [R("coord"), R("kk%d" % t)], [R("na%d" % t)])
+
+    def dist_tail(t):
+        a = 20 + 8 * t
+        add("S", lambda: S.activation(T["abt%d" % t][:], T.ccf[:, a:a + 8], ACT.Abs, bias=T["na%d" % t][:, 0:1]),
+            [R("ccf"), R("na%d" % t)], [R("abt%d" % t)])
+
+    def dist_own(t, f):
+        add("S", lambda: S.activation(T["abe%d" % t][:, 10 * f:10 * f + 10], T.ccf[:, 10 * f:10 * f + 10], ACT.Abs,
+                                      bias=T["na%d" % t][:, 16 + 16 * f:17 + 16 * f]),
+            [R("ccf"), R("na%d" % t)], [R("abe%d" % t, 10 * f, 10 * f + 10)])
+
+    def sign(t):
+        cs = T["cs%d" % t]
+        add("V", lambda: V.tensor_scalar(cs[:, 0:1], T.ps[:, 512 * 5:512 * 5 + 1], 0.0, 0.5, ALU.is_gt, ALU.subtract),
+            [bank(5)], [R("cs%d" % t, 0, 1)])
+
+    def size(t):
+        return 1.0 if t == 0 else 0.015625
+
+    def sign_scaled(t, col, s):
+        cs = T["cs%d" % t]
+        add("S", lambda: S.activation(cs[:, col:col + 1], cs[:, 0:1], ACT.Copy, scale=s * size(t)),
+            [R("cs%d" % t, 0, 1)], [R("cs%d" % t, col, col + 1)])
+
+    def offs_tail(t):
+        abt, oft = T["abt%d" % t], T["oft%d" % t]
+        if t == 0:
+            for b in (2, 3, 0, 1):
+                add("V", lambda b=b: V.tensor_scalar(oft[:, 8 * b:8 * b + 8], abt[:], 4.0, float(b), ALU.mult, ALU.add),
+                    [R("abt%d" % t)], [R("oft%d" % t, 8 * b, 8 * b + 8)])
+        else:
+            add("V", lambda: V.tensor_copy(oft[:, 0:8], abt[:]), [R("abt%d" % t)], [R("oft%d" % t, 0, 8)])
+
+    def tail(t, b):
+        cs, gt, oft = T["cs%d" % t], T["gt%d" % t], T["oft%d" % t]
+        if t == 0:
+            src = lambda: T.bms[:].indirect(oft[:, 8 * b:8 * b + 8])
+            rd = [R("bms"), R("oft0", 8 * b, 8 * b + 8)]
+        else:
+            src = lambda: T["bp%d" % t][:, C * b:C * b + C].indirect(oft[:, 0:8])
+            rd = [R("bp%d" % t, plane=b), R("oft%d" % t, 0, 8)]
+        out = gt[:, b:4 * TL:4]
+        if b < 2:
+            add("V", lambda: V.tensor_scalar(out, src(), cs[:, 0:1], size(t), ALU.mult, ALU.mult),
+                rd + [R("cs%d" % t, 0, 1)], [R("gt%d" % t, plane=b)])
+        else:
+            col = 0 if t == 0 else 1
+            add("S", lambda: S.activation(out, src(), ACT.Copy, scale=cs[:, col:col + 1]),
+                rd + [R("cs%d" % t, col, col + 1)], [R("gt%d" % t, plane=b)])
+
+    def send(t):
+        dst = T.cores[(rank + STEP[t]) % n_ranks]
+        rid, pid, _ = topo.addr(dst)
+        m = topo.mask(core, dst)
+        arr = T.sem["arr%d" % t]
+        add("G", lambda: g.remote_dma(T["lq%d" % t][:].bitcast(dt.uint8), T["qg%d" % t][:].bitcast(dt.uint8),
+                                      arr, T.sem.loc, pid, rid, m), [R("qg%d" % t)], [])
+        add("G", lambda: g.remote_dma(T["ls%d" % t][:], T["sg%d" % t][:], arr, T.sem.loc, pid, rid, m),
+            [R("sg%d" % t)], [])
+        return 2 * len(topo.engines(core, dst))
+
+    def window(t, b):
+        cs, win = T["cs%d" % t], T["win%d" % t]
+        if t == 0:
+            src, rd = T.bms[:, b:4 * C:4], [R("bms")]
+        else:
+            src, rd = T["bp%d" % t][:, C * b:C * b + C], [R("bp%d" % t, plane=b)]
+        out = win[:, C * b:C * b + C]
+        if b == 0:
+            add("V", lambda: V.tensor_scalar(out, src, cs[:, 0:1], -size(t), ALU.mult, ALU.mult),
+                rd + [R("cs%d" % t, 0, 1)], [R("win%d" % t, plane=b)])
+        else:
+            add("S", lambda: S.activation(out, src, ACT.Copy, scale=cs[:, 2:3]),
+                rd + [R("cs%d" % t, 2, 3)], [R("win%d" % t, plane=b)])
+
+    def subtract(t, b, late):
+        win, ofe, x, xn = T["win%d" % t], T["ofe%d" % t], T["xs%d" % t], T["xs%d" % (t + 1)]
+        rd = [R("win%d" % t, plane=b), R("ofe%d" % t)]
+        if late:
+            add("V", lambda: V.tensor_tensor(T["el%d" % t][:, TL * b:TL * b + TL],
+                                             win[:, C * b:C * b + C].indirect(ofe[:, 0:8]), x[:, b:4 * TL:4], ALU.add),
+                rd + [R("xs%d" % t, 0, TL, b)], [R("el%d" % t, plane=b)])
+        else:
+            add("V", lambda: V.tensor_tensor(xn[:, 4 * TL + b:4 * C:4],
+                                             win[:, C * b:C * b + C].indirect(ofe[:, 8:20]), x[:, 4 * TL + b:4 * C:4], ALU.add),
+                rd + [R("xs%d" % t, TL, C, b)], [R("xs%d" % (t + 1), TL, C, b)])
+
+    def arrived(t, b):
+        xn = T["xs%d" % (t + 1)]
+        add("V", lambda: V.tensor_tensor(xn[:, b:4 * TL:4], T["el%d" % t][:, TL * b:TL * b + TL],
+                                         T.ps[:, 512 * b:512 * b + TL], ALU.subtract),
+            [R("el%d" % t, plane=b), bank(b)], [R("xs%d" % (t + 1), 0, TL, b)])
+
+    def beam(t, b, late):
+        a, e = (0, TL) if late else (TL, C)
+        k = b if late else 4 + b
+        aux = T["aux%d" % t]
+        old = aux[:, 4 * a + b:4 * e:4] if t == 0 else aux[:, C * b + a:C * b + e]
+        add("V", lambda: V.tensor_tensor(T["bp%d" % (t + 1)][:, C * b + a:C * b + e], T.ps[:, 512 * k:512 * k + e - a],
+                                         old, ALU.add),
+            [bank(k), R("aux%d" % t)], [R("bp%d" % (t + 1), a, e, b)])
+
+    def beam_col0(t, b):
+        add("S", lambda: S.activation(T.z[:, b:b + 1], T.ps[:, 512 * b:512 * b + 1], ACT.Identity,
+                                      bias=T.hcol[:, 4 * t + b:4 * t + b + 1], scale=0.015625),
+            [bank(b), R("hcol", 4 * t, 4 * t + 4)], [R("z", b, b + 1)])
+
+    def quant_z(t):
+        quant("qz%d" % t, "sz%d" % t, 0, 128, T.z[:], [R("z")])
+
+    add("Y", lambda: Y.dma_start(T.us[:], T.u[:]), [], [R("us")], sem="lu")
+    add("S", lambda: S.dma_start(T.z[:, 0:8], T.bm[:, 0:8]), [], [R("z", 0, 8)], sem="lz")
+    add("Y", lambda: Y.dma_start(T.xs0[:, 4 * HALF:4 * C], T.x[:, 4 * HALF:4 * C]), [], [R("xs0", HALF, C)], sem="lx1")
+    add("S", lambda: S.dma_start(T.cc[:, 0:20], T.co[:]), [], [R("cc", 0, 20)], sem="lcc")
+    add("Y", lambda: Y.dma_start(T.xs0[:, 0:4 * HALF], T.x[:, 0:4 * HALF]), [], [R("xs0", 0, HALF)], sem="lx0")
+    add("S", lambda: S.dma_start(T.cc[:, 20:44], T.cn[:]), [], [R("cc", 20, 44)], sem="lcc")
+    add("Y", lambda: Y.dma_start(T.bms[:], T.bm[:]), [], [R("bms")], sem="lbm")
+    add("Y", lambda: Y.dma_start(T.wq[:].bitcast(dt.uint8), T.wc[:]), [], [R("wq")], sem="lw")
+    add("Y", lambda: Y.dma_start(T.wsc[:], T.ws[:]), [], [R("wsc")], sem="lw")
+
+    add("G", lambda: g.iota(T.jp[:], [[1, 128]], 0, -1, allow_small_or_imprecise_dtypes=True), [], [R("jp")])
+    add("G", lambda: g.iota(T.uo32[:], [[16, 8]], 0, 0), [], [R("uo32")])
+    add("G", lambda: g.iota(T.ramp[:], [[1, C]], 0, 0, allow_small_or_imprecise_dtypes=True), [], [R("ramp")])
+    add("V", lambda: V.memset(T.band[:], 0.0), [], [R("band")])
+    add("V", lambda: V.memset(T.z[:, 8:512], 0.0), [], [R("z", 8, 512)])
+    add("V", lambda: V.tensor_scalar(T.band[:, 3:515:4], T.jp[:], 0.0, None, ALU.is_equal), [R("jp")], [R("band")])
+    add("V", lambda: V.memset(T.neg[:], LOW), [], [R("neg")])
+    add("V", lambda: V.tensor_copy(T.uo16[:], T.uo32[:]), [R("uo32")], [R("uo16")])
+    for b in range(4):
+        quant("qe", "se", 128 * b, 128 * b + 128, T.band[:, 3 - b:515 - b], [R("band")])
+
+    quant("qu", "su", 0, 128, T.us[:], [R("us")])
+    quant_z(0)
+    add("V", lambda: V.tensor_copy(T.qur[:].bitcast(dt.uint32), T.qu[:].bitcast(dt.uint32).indirect(T.uo16[:])),
+        [R("qu"), R("uo16")], [R("qur")])
+    add("S", lambda: S.activation(T.sur[:], T.su[:].indirect(T.uo16[:]), ACT.Copy), [R("su"), R("uo16")], [R("sur")])
+    mm(5, "qur", "sur", 0, "qz0", "sz0", 0, 128)
+    quant_x(0, HALF, C)
+    add("V", lambda: V.tensor_copy(T.co16[:], T.cc[:, 0:20]), [R("cc")], [R("co16")])
+    add("V", lambda: V.tensor_copy(T.ccf[:], T.cc[:]), [R("cc")], [R("ccf")])
+    add("S", lambda: S.activation(T.coord[:], T.ramp[:].indirect(T.co16[:]), ACT.Copy), [R("ramp"), R("co16")], [R("coord")])
+    mm(4, "qur", "sur", 0, "qx0", "sx0", HALF, C)
+    sign(0)
+    quant_x(0, 0, HALF)
+    mm(6, "qur", "sur", 0, "qx0", "sx0", 0, HALF)
+    sign_scaled(0, 2, -1.0)
+    scan(0, 1, 4)
+    count(0, 1)
+    scan(0, 0, 6)
+    count(0, 0)
+    peak1(0, "V")
+    higher(0)
+    peaks16(0)
+    peak_coords(0)
+    dist_tail(0)
+    offs_tail(0)
+    dist_own(0, 0)
+    dist_own(0, 1)
+
+    sent = 0
+    for t in range(ROUNDS):
+        last = t == ROUNDS - 1
+        qn, sn = "qx%d" % (t + 1), "sx%d" % (t + 1)
+        store_peaks(t)
+        for b in (2, 0, 3, 1):
+            tail(t, b)
+        quant("qg%d" % t, "sg%d" % t, 0, TL, T["gt%d" % t][:], [R("gt%d" % t)])
+        sent += send(t)
+        src = T.cores[(rank - STEP[t]) % n_ranks]
+        landed = 2 * len(topo.engines(src, core))
+        add("V", lambda t=t: V.tensor_copy(T["ofe%d" % t][:], T["abe%d" % t][:]), [R("abe%d" % t)], [R("ofe%d" % t)])
+        if t > 0:
+            sign_scaled(t, 2, -1.0)
+        for b in range(4):
+            window(t, b)
+        if not last:
+            if t == 0:
+                add("S", lambda: S.activation(T.aux0[:], T.bms[:], ACT.Copy, scale=32.0), [R("bms")], [R("aux0")])
+            else:
+                add("S", lambda t=t: S.activation(T["aux%d" % t][:], T["bp%d" % t][:], ACT.Copy, scale=0.5),
+                    [R("bp%d" % t)], [R("aux%d" % t)])
+            add("S", lambda t=t: S.activation(T.hcol[:, 4 * t:4 * t + 4], T.z[:, 0:4], ACT.Copy, scale=0.5),
+                [R("z", 0, 4)], [R("hcol", 4 * t, 4 * t + 4)])
+        for b in range(4):
+            subtract(t, b, False)
+        quant_x(t + 1, TL, C)
+        if not last:
+            mm(0, "qur", "sur", 0, qn, sn, HALF, C)
+            for b in range(4):
+                mm(4 + b, "wq", "wsc", 128 * b, qn, sn, TL, C)
+        else:
+            add("Y", lambda: Y.dma_start(T.oc[:, 4 * TL:4 * C], T[qn][:, TL:C].bitcast(dt.uint8)), [R(qn, TL, C)], [], sem="sty")
+            quant("qv", "sv", 0, 128, T.vs[:], [R("vs")])
+            mm(4, "qv", "sv", 0, qn, sn, TL, C)
+            add("S", lambda: S.activation(T.ysb[:, TL:C], T.ps[:, 512 * 4:512 * 4 + C - TL], ACT.Copy),
+                [bank(4)], [R("ysb", TL, C)])
+            add("Y", lambda: Y.dma_start(T.y[:, TL:C], T.ysb[:, TL:C]), [R("ysb", TL, C)], [], sem="sty")
+        for b in range(4):
+            subtract(t, b, True)
+        if not last:
+            scan(t + 1, 1, 0)
+            count(t + 1, 1)
+            peak1(t + 1, "S")
+            for b in range(3):
+                beam(t, b, False)
+        order = (1, 2, 3, 0)
+        for b in order:
+            mm(b, "qe", "se", 128 * b, "lq%d" % t, "ls%d" % t, 0, TL,
+               ext=[("arr%d" % t, landed)] if b == order[0] else [])
+        for b in order:
+            arrived(t, b)
+        quant_x(t + 1, 0, TL)
+        if last:
+            break
+        if t == 0:
+            add("Y", lambda: Y.dma_start(T.vs[:], T.v[:]), [R("xs1", 0, TL, order[0])], [R("vs")], sem="lv")
+        mm(4, "qur", "sur", 0, qn, sn, 0, HALF)
+        for b in range(4):
+            mm(b, "wq", "wsc", 128 * b, qn, sn, 0, TL)
+        beam(t, 3, False)
+        scan(t + 1, 0, 4)
+        beam_col0(t, 0)
+        beam_col0(t, 1)
+        count(t + 1, 0)
+        beam_col0(t, 2)
+        beam_col0(t, 3)
+        higher(t + 1)
+        beam(t, 0, True)
+        beam(t, 1, True)
+        peaks16(t + 1)
+        quant_z(t + 1)
+        mm(5, "qur", "sur", 0, "qz%d" % (t + 1), "sz%d" % (t + 1), 0, 128)
+        peak_coords(t + 1)
+        beam(t, 2, True)
+        beam(t, 3, True)
+        dist_tail(t + 1)
+        dist_own(t + 1, 0)
+        dist_own(t + 1, 1)
+        sign(t + 1)
+        offs_tail(t + 1)
+        sign_scaled(t + 1, 1, 1.0)
+
+    qn, sn = "qx%d" % ROUNDS, "sx%d" % ROUNDS
+    mm(5, "qv", "sv", 0, qn, sn, 0, TL)
+    add("Y", lambda: Y.dma_start(T.oc[:, 0:4 * TL], T[qn][:, 0:TL].bitcast(dt.uint8)), [R(qn, 0, TL)], [], sem="sty")
+    for k in range(4):
+        q, e, sem = ("Y", Y, "sty") if k == 0 else ("S", S, "sts")
+        add(q, lambda k=k, e=e: e.dma_start(T.osc[4 * k:4 * k + 4, :], T[sn][32 * k:32 * k + 4, :]), [R(sn)], [], sem=sem)
+    add("V", lambda: V.tensor_copy(T.ysb[:, 0:TL], T.ps[:, 512 * 5:512 * 5 + TL]), [bank(5)], [R("ysb", 0, TL)])
+    add("Y", lambda: Y.dma_start(T.y[:, 0:TL], T.ysb[:, 0:TL]), [R("ysb", 0, TL)], [], sem="sty")
+
+    emit(g, T, ops, [("G", "loc", sent), ("Y", "sty", None), ("S", "sts", None)])

@@ -4,12 +4,18 @@ ALU = AluOpType
 ACT = ActivationFunctionType
 C, TL, ROUNDS = 320, 128, 3
 HALF = C // 2
+CUT = 72
+LATE = 48
+EARLY = [(128, 224), (224, 320)]
+EARLY_BANK = [5, 6, 4, 7]
 STEP = [1, 2, 1]
 LOW = -9.0e29
+TINY = 2.0 ** -120
 CODES, PLANE = "float8_e4m3fn_x4", "uint8"
+NO, NT = C // 4, TL // 4
 
 SCRATCH = {
-    "bms": ("sbuf", [128, 4 * C], "bfloat16"),
+    "bt0": ("sbuf", [128, 4 * C], "bfloat16"),
     "us": ("sbuf", [128, 512], "bfloat16"),
     "vs": ("sbuf", [128, 512], "bfloat16"),
     "qu": ("sbuf", [128, 128], CODES), "su": ("sbuf", [128, 128], PLANE),
@@ -17,12 +23,15 @@ SCRATCH = {
     "qv": ("sbuf", [128, 128], CODES), "sv": ("sbuf", [128, 128], PLANE),
     "wq": ("sbuf", [128, 512], CODES), "wsc": ("sbuf", [128, 512], PLANE),
     "qe": ("sbuf", [128, 512], CODES), "se": ("sbuf", [128, 512], PLANE),
-    "cc": ("sbuf", [128, 44], "int32"), "ccf": ("sbuf", [128, 44], "float32"),
-    "co16": ("sbuf", [128, 20], "uint16"),
-    "uo32": ("sbuf", [128, 8], "int32"), "uo16": ("sbuf", [128, 8], "uint16"),
+    "cc": ("sbuf", [128, 44], "int32"), "co16": ("sbuf", [128, 20], "uint16"),
+    "c4": ("sbuf", [128, 64], "float32"), "c4t": ("sbuf", [128, 64], "float32"),
+    "c4h": ("sbuf", [128, 256], "float32"), "c4u": ("sbuf", [128, 256], "float32"),
+    "tab": ("sbuf", [128, 176], "float32"),
+    "pi": ("sbuf", [128, 4], "int32"), "pf": ("sbuf", [128, 4], "float32"),
+    "lf": ("sbuf", [128, 40], "float32"), "l16": ("sbuf", [128, 40], "uint16"),
     "jp": ("sbuf", [128, 128], "bfloat16"), "band": ("sbuf", [128, 520], "bfloat16"),
     "ramp": ("sbuf", [128, C], "float32"), "coord": ("sbuf", [128, C], "float32"),
-    "neg": ("sbuf", [128, HALF], "float32"),
+    "nil": ("sbuf", [128, HALF], "float32"), "tiny": ("sbuf", [128, 4], "float32"),
     "z": ("sbuf", [128, 512], "bfloat16"),
     "hcol": ("sbuf", [128, 8], "float32"),
     "junk": ("sbuf", [128, C], "float32"),
@@ -38,12 +47,10 @@ for _t in range(ROUNDS):
     SCRATCH["yk%d" % _t] = ("sbuf", [128, 4], "float32")
     SCRATCH["kk%d" % _t] = ("sbuf", [128, 4], "uint16")
     SCRATCH["na%d" % _t] = ("sbuf", [128, 48], "float32")
-    SCRATCH["abt%d" % _t] = ("sbuf", [128, 8], "float32")
-    SCRATCH["abe%d" % _t] = ("sbuf", [128, 20], "float32")
-    SCRATCH["oft%d" % _t] = ("sbuf", [128, 32], "uint16")
-    SCRATCH["ofe%d" % _t] = ("sbuf", [128, 20], "uint16")
+    SCRATCH["ab%d" % _t] = ("sbuf", [128, NT + NO], "float32")
+    SCRATCH["of%d" % _t] = ("sbuf", [128, NT + NO], "uint16")
     SCRATCH["cs%d" % _t] = ("sbuf", [128, 4], "float32")
-    SCRATCH["win%d" % _t] = ("sbuf", [128, 4 * C], "bfloat16")
+    SCRATCH["ge%d" % _t] = ("sbuf", [128, 4 * C], "bfloat16")
     SCRATCH["gt%d" % _t] = ("sbuf", [128, 4 * TL], "bfloat16")
     SCRATCH["qg%d" % _t] = ("sbuf", [128, TL], CODES)
     SCRATCH["sg%d" % _t] = ("sbuf", [128, TL], PLANE)
@@ -54,9 +61,9 @@ for _t in range(ROUNDS):
     SCRATCH["el%d" % _t] = ("sbuf", [128, 4 * TL], "float32")
 for _t in range(ROUNDS - 1):
     SCRATCH["aux%d" % _t] = ("sbuf", [128, 4 * C], "bfloat16")
-    SCRATCH["bp%d" % (_t + 1)] = ("sbuf", [128, 4 * C], "bfloat16")
+    SCRATCH["bt%d" % (_t + 1)] = ("sbuf", [128, 4 * C], "bfloat16")
 
-SEMAPHORES = ["cv", "cs", "cp", "cg", "lu", "lx0", "lx1", "lbm", "lz", "lcc", "lw", "lv",
+SEMAPHORES = ["cv", "cs", "cp", "cg", "lu", "lx0", "lx1", "lb0", "lb1", "lcc", "lw", "lv",
               "sty", "sts", "arr0", "arr1", "arr2", "loc"]
 COUNTER = {"V": "cv", "S": "cs", "P": "cp", "G": "cg"}
 
@@ -166,14 +173,18 @@ def rank_program(g, core, T, topo):
                                      T[rq][:, a:b], T[rs][:, a:b], True, True),
             [R(lq, la, la + 128), R(ls, la, la + 128), R(rq, a, b), R(rs, a, b)], [bank(k)], ext=ext)
 
+    def iota(name, a, b, pattern, per_partition, whole=False):
+        flag = {} if whole else {"allow_small_or_imprecise_dtypes": True}
+        add("G", lambda: g.iota(T[name][:, a:b], pattern, 0, per_partition, **flag), [], [R(name, a, b)])
+
     def quant_x(t, a, b):
         quant("qx%d" % t, "sx%d" % t, a, b, T["xs%d" % t][:, 4 * a:4 * b], [R("xs%d" % t, a, b)])
 
     def scan(t, f, k):
         run = T["run%d" % t]
         add("V", lambda: V.tensor_tensor_scan(run[:, HALF * f:HALF * f + HALF], T.ps[:, 512 * k:512 * k + HALF],
-                                              T.neg[:], LOW, ALU.max, ALU.max),
-            [bank(k), R("neg")], [R("run%d" % t, HALF * f, HALF * f + HALF)])
+                                              T.nil[:], LOW, ALU.max, ALU.add),
+            [bank(k), R("nil")], [R("run%d" % t, HALF * f, HALF * f + HALF)])
 
     def count(t, f):
         run, yk = T["run%d" % t], T["yk%d" % t]
@@ -183,13 +194,10 @@ def rank_program(g, core, T, topo):
                                       accum_out=yk[:, col:col + 1]),
             [R("run%d" % t, a, b)], [R("junk", a, b), R("yk%d" % t, col, col + 1)])
 
-    def peak1(t, q):
+    def peak1(t):
         yk = T["yk%d" % t]
-        if q == "V":
-            f = lambda: V.tensor_scalar(yk[:, 2:3], yk[:, 3:4], float(HALF), None, ALU.add)
-        else:
-            f = lambda: S.activation(yk[:, 2:3], yk[:, 3:4], ACT.Identity, bias=T.ramp[:, HALF:HALF + 1])
-        add(q, f, [R("yk%d" % t, 3, 4), R("ramp")], [R("yk%d" % t, 2, 3)])
+        add("S", lambda: S.activation(yk[:, 2:3], yk[:, 3:4], ACT.Identity, bias=T.ramp[:, HALF:HALF + 1]),
+            [R("yk%d" % t, 3, 4), R("ramp")], [R("yk%d" % t, 2, 3)])
 
     def higher(t):
         run, yk = T["run%d" % t], T["yk%d" % t]
@@ -207,57 +215,40 @@ def rank_program(g, core, T, topo):
         add("Y", lambda: Y.dma_start(T.ol[:, 2 * t:2 * t + 2], yk[0:128:16, 1:3]), [R("yk%d" % t, 1, 3)], [], sem="sty")
 
     def peak_coords(t):
-        add("S", lambda: S.activation(T["na%d" % t][:], T.coord[:].indirect(T["kk%d" % t][:, 0:3]), ACT.Copy, scale=-1.0),
+        add("S", lambda: S.activation(T["na%d" % t][:], T.coord[:].indirect(T["kk%d" % t][:, 0:3]), ACT.Copy, scale=-4.0),
             [R("coord"), R("kk%d" % t)], [R("na%d" % t)])
 
-    def dist_tail(t):
-        a = 20 + 8 * t
-        add("S", lambda: S.activation(T["abt%d" % t][:], T.ccf[:, a:a + 8], ACT.Abs, bias=T["na%d" % t][:, 0:1]),
-            [R("ccf"), R("na%d" % t)], [R("abt%d" % t)])
+    def dist(t, e):
+        a, n, to = [(NO + NT * t, NT, 0), (0, NO // 2, NT), (NO // 2, NO // 2, NT + NO // 2)][e]
+        add("S", lambda: S.activation(T["ab%d" % t][:, to:to + n], T.tab[:, a:a + n], ACT.Abs,
+                                      bias=T["na%d" % t][:, 16 * e:16 * e + 1]),
+            [R("tab"), R("na%d" % t)], [R("ab%d" % t, to, to + n)])
 
-    def dist_own(t, f):
-        add("S", lambda: S.activation(T["abe%d" % t][:, 10 * f:10 * f + 10], T.ccf[:, 10 * f:10 * f + 10], ACT.Abs,
-                                      bias=T["na%d" % t][:, 16 + 16 * f:17 + 16 * f]),
-            [R("ccf"), R("na%d" % t)], [R("abe%d" % t, 10 * f, 10 * f + 10)])
-
-    def sign(t):
-        cs = T["cs%d" % t]
-        add("V", lambda: V.tensor_scalar(cs[:, 0:1], T.ps[:, 512 * 5:512 * 5 + 1], 0.0, 0.5, ALU.is_gt, ALU.subtract),
-            [bank(5)], [R("cs%d" % t, 0, 1)])
+    def offsets(t):
+        add("V", lambda: V.tensor_scalar(T["of%d" % t][:], T["ab%d" % t][:], T.pf[:, 1:2], None, ALU.add),
+            [R("ab%d" % t), R("pf")], [R("of%d" % t)])
 
     def size(t):
         return 1.0 if t == 0 else 0.015625
 
-    def sign_scaled(t, col, s):
+    def sign(t):
         cs = T["cs%d" % t]
-        add("S", lambda: S.activation(cs[:, col:col + 1], cs[:, 0:1], ACT.Copy, scale=s * size(t)),
-            [R("cs%d" % t, 0, 1)], [R("cs%d" % t, col, col + 1)])
+        add("S", lambda: S.activation(cs[:, 0:1], T.ps[:, 512 * 5:512 * 5 + 1], ACT.Sign, bias=T.tiny[:, 0:1]),
+            [bank(5), R("tiny")], [R("cs%d" % t, 0, 1)])
+        add("S", lambda: S.activation(cs[:, 1:2], cs[:, 0:1], ACT.Copy, scale=0.5 * size(t)),
+            [R("cs%d" % t, 0, 1)], [R("cs%d" % t, 1, 2)])
 
-    def offs_tail(t):
-        abt, oft = T["abt%d" % t], T["oft%d" % t]
-        if t == 0:
-            for b in (2, 3, 0, 1):
-                add("V", lambda b=b: V.tensor_scalar(oft[:, 8 * b:8 * b + 8], abt[:], 4.0, float(b), ALU.mult, ALU.add),
-                    [R("abt%d" % t)], [R("oft%d" % t, 8 * b, 8 * b + 8)])
+    def gather(t, q, name, a, b, first):
+        cs, of, bt = T["cs%d" % t], T["of%d" % t], T["bt%d" % t]
+        la, lb = first + a // 4, first + b // 4
+        out = T[name][:, 4 * a:4 * b]
+        if q == "S":
+            add("S", lambda: S.activation(out, bt[:].indirect(of[:, la:lb]), ACT.Copy, scale=cs[:, 1:2]),
+                [R("bt%d" % t), R("of%d" % t, la, lb), R("cs%d" % t, 1, 2)], [R(name, a, b)])
         else:
-            add("V", lambda: V.tensor_copy(oft[:, 0:8], abt[:]), [R("abt%d" % t)], [R("oft%d" % t, 0, 8)])
-
-    def tail(t, b):
-        cs, gt, oft = T["cs%d" % t], T["gt%d" % t], T["oft%d" % t]
-        if t == 0:
-            src = lambda: T.bms[:].indirect(oft[:, 8 * b:8 * b + 8])
-            rd = [R("bms"), R("oft0", 8 * b, 8 * b + 8)]
-        else:
-            src = lambda: T["bp%d" % t][:, C * b:C * b + C].indirect(oft[:, 0:8])
-            rd = [R("bp%d" % t, plane=b), R("oft%d" % t, 0, 8)]
-        out = gt[:, b:4 * TL:4]
-        if b < 2:
-            add("V", lambda: V.tensor_scalar(out, src(), cs[:, 0:1], size(t), ALU.mult, ALU.mult),
-                rd + [R("cs%d" % t, 0, 1)], [R("gt%d" % t, plane=b)])
-        else:
-            col = 0 if t == 0 else 1
-            add("S", lambda: S.activation(out, src(), ACT.Copy, scale=cs[:, col:col + 1]),
-                rd + [R("cs%d" % t, col, col + 1)], [R("gt%d" % t, plane=b)])
+            add("V", lambda: V.tensor_scalar(out, bt[:].indirect(of[:, la:lb]), cs[:, 0:1], 0.5 * size(t),
+                                             ALU.mult, ALU.mult),
+                [R("bt%d" % t), R("of%d" % t, la, lb), R("cs%d" % t, 0, 1)], [R(name, a, b)])
 
     def send(t):
         dst = T.cores[(rank + STEP[t]) % n_ranks]
@@ -270,186 +261,182 @@ def rank_program(g, core, T, topo):
             [R("sg%d" % t)], [])
         return 2 * len(topo.engines(core, dst))
 
-    def window(t, b):
-        cs, win = T["cs%d" % t], T["win%d" % t]
-        if t == 0:
-            src, rd = T.bms[:, b:4 * C:4], [R("bms")]
-        else:
-            src, rd = T["bp%d" % t][:, C * b:C * b + C], [R("bp%d" % t, plane=b)]
-        out = win[:, C * b:C * b + C]
-        if b == 0:
-            add("V", lambda: V.tensor_scalar(out, src, cs[:, 0:1], -size(t), ALU.mult, ALU.mult),
-                rd + [R("cs%d" % t, 0, 1)], [R("win%d" % t, plane=b)])
-        else:
-            add("S", lambda: S.activation(out, src, ACT.Copy, scale=cs[:, 2:3]),
-                rd + [R("cs%d" % t, 2, 3)], [R("win%d" % t, plane=b)])
-
-    def subtract(t, b, late):
-        win, ofe, x, xn = T["win%d" % t], T["ofe%d" % t], T["xs%d" % t], T["xs%d" % (t + 1)]
-        rd = [R("win%d" % t, plane=b), R("ofe%d" % t)]
-        if late:
-            add("V", lambda: V.tensor_tensor(T["el%d" % t][:, TL * b:TL * b + TL],
-                                             win[:, C * b:C * b + C].indirect(ofe[:, 0:8]), x[:, b:4 * TL:4], ALU.add),
-                rd + [R("xs%d" % t, 0, TL, b)], [R("el%d" % t, plane=b)])
-        else:
-            add("V", lambda: V.tensor_tensor(xn[:, 4 * TL + b:4 * C:4],
-                                             win[:, C * b:C * b + C].indirect(ofe[:, 8:20]), x[:, 4 * TL + b:4 * C:4], ALU.add),
-                rd + [R("xs%d" % t, TL, C, b)], [R("xs%d" % (t + 1), TL, C, b)])
+    def subtract(t, a, b):
+        name = "el%d" % t if b <= TL else "xs%d" % (t + 1)
+        add("V", lambda: V.tensor_tensor(T[name][:, 4 * a:4 * b], T["xs%d" % t][:, 4 * a:4 * b],
+                                         T["ge%d" % t][:, 4 * a:4 * b], ALU.subtract),
+            [R("xs%d" % t, a, b), R("ge%d" % t, a, b)], [R(name, a, b)])
 
     def arrived(t, b):
         xn = T["xs%d" % (t + 1)]
-        add("V", lambda: V.tensor_tensor(xn[:, b:4 * TL:4], T["el%d" % t][:, TL * b:TL * b + TL],
+        add("V", lambda: V.tensor_tensor(xn[:, b:4 * TL:4], T["el%d" % t][:, b:4 * TL:4],
                                          T.ps[:, 512 * b:512 * b + TL], ALU.subtract),
-            [R("el%d" % t, plane=b), bank(b)], [R("xs%d" % (t + 1), 0, TL, b)])
+            [R("el%d" % t), bank(b)], [R("xs%d" % (t + 1), 0, TL, b)])
+
+    def halve(t, a, e):
+        add("S", lambda: S.activation(T["aux%d" % t][:, 4 * a:4 * e], T["bt%d" % t][:, 4 * a:4 * e], ACT.Copy,
+                                      scale=32.0 * size(t)),
+            [R("bt%d" % t, a, e)], [R("aux%d" % t, a, e)])
+
+    def layer(t, b, late):
+        a, e = (0, TL) if late else (TL, C)
+        mm(b if late else EARLY_BANK[b], "wq", "wsc", 128 * b, "qx%d" % (t + 1), "sx%d" % (t + 1), a, e)
 
     def beam(t, b, late):
         a, e = (0, TL) if late else (TL, C)
-        k = b if late else 4 + b
-        aux = T["aux%d" % t]
-        old = aux[:, 4 * a + b:4 * e:4] if t == 0 else aux[:, C * b + a:C * b + e]
-        add("V", lambda: V.tensor_tensor(T["bp%d" % (t + 1)][:, C * b + a:C * b + e], T.ps[:, 512 * k:512 * k + e - a],
-                                         old, ALU.add),
-            [bank(k), R("aux%d" % t)], [R("bp%d" % (t + 1), a, e, b)])
+        k = b if late else EARLY_BANK[b]
+        add("V", lambda: V.tensor_tensor(T["bt%d" % (t + 1)][:, 4 * a + b:4 * e:4], T.ps[:, 512 * k:512 * k + e - a],
+                                         T["aux%d" % t][:, 4 * a + b:4 * e:4], ALU.add),
+            [bank(k), R("aux%d" % t, a, e)], [R("bt%d" % (t + 1), a, e, b)])
 
     def beam_col0(t, b):
         add("S", lambda: S.activation(T.z[:, b:b + 1], T.ps[:, 512 * b:512 * b + 1], ACT.Identity,
                                       bias=T.hcol[:, 4 * t + b:4 * t + b + 1], scale=0.015625),
             [bank(b), R("hcol", 4 * t, 4 * t + 4)], [R("z", b, b + 1)])
 
-    def quant_z(t):
-        quant("qz%d" % t, "sz%d" % t, 0, 128, T.z[:], [R("z")])
-
     add("Y", lambda: Y.dma_start(T.us[:], T.u[:]), [], [R("us")], sem="lu")
-    add("S", lambda: S.dma_start(T.z[:, 0:8], T.bm[:, 0:8]), [], [R("z", 0, 8)], sem="lz")
-    add("Y", lambda: Y.dma_start(T.xs0[:, 4 * HALF:4 * C], T.x[:, 4 * HALF:4 * C]), [], [R("xs0", HALF, C)], sem="lx1")
     add("S", lambda: S.dma_start(T.cc[:, 0:20], T.co[:]), [], [R("cc", 0, 20)], sem="lcc")
-    add("Y", lambda: Y.dma_start(T.xs0[:, 0:4 * HALF], T.x[:, 0:4 * HALF]), [], [R("xs0", 0, HALF)], sem="lx0")
     add("S", lambda: S.dma_start(T.cc[:, 20:44], T.cn[:]), [], [R("cc", 20, 44)], sem="lcc")
-    add("Y", lambda: Y.dma_start(T.bms[:], T.bm[:]), [], [R("bms")], sem="lbm")
+    add("Y", lambda: Y.dma_start(T.xs0[:, 4 * HALF:4 * C], T.x[:, 4 * HALF:4 * C]), [], [R("xs0", HALF, C)], sem="lx1")
+    add("Y", lambda: Y.dma_start(T.xs0[:, 0:4 * HALF], T.x[:, 0:4 * HALF]), [], [R("xs0", 0, HALF)], sem="lx0")
+    add("Y", lambda: Y.dma_start(T.bt0[:, 0:4 * TL], T.bm[:, 0:4 * TL]), [], [R("bt0", 0, TL)], sem="lb0")
+    add("Y", lambda: Y.dma_start(T.bt0[:, 4 * TL:4 * C], T.bm[:, 4 * TL:4 * C]), [], [R("bt0", TL, C)], sem="lb1")
     add("Y", lambda: Y.dma_start(T.wq[:].bitcast(dt.uint8), T.wc[:]), [], [R("wq")], sem="lw")
     add("Y", lambda: Y.dma_start(T.wsc[:], T.ws[:]), [], [R("wsc")], sem="lw")
 
-    add("G", lambda: g.iota(T.jp[:], [[1, 128]], 0, -1, allow_small_or_imprecise_dtypes=True), [], [R("jp")])
-    add("G", lambda: g.iota(T.uo32[:], [[16, 8]], 0, 0), [], [R("uo32")])
-    add("G", lambda: g.iota(T.ramp[:], [[1, C]], 0, 0, allow_small_or_imprecise_dtypes=True), [], [R("ramp")])
+    iota("pi", 0, 1, [[0, 1]], 1, whole=True)
+    iota("jp", 0, 128, [[1, 128]], -1)
+    iota("lf", 0, 8, [[16, 8]], 0)
+    iota("lf", 8, 24, [[32, 2], [4, 4], [16, 2]], 0)
+    iota("c4", 44, 64, [[0, 20]], 0)
+    iota("lf", 24, 40, [[128, 2], [4, 8]], 0)
+    iota("ramp", 0, C, [[1, C]], 0)
+    iota("nil", 0, HALF, [[0, HALF]], 0)
+    iota("z", 4, 512, [[0, 508]], 0)
     add("V", lambda: V.memset(T.band[:], 0.0), [], [R("band")])
-    add("V", lambda: V.memset(T.z[:, 8:512], 0.0), [], [R("z", 8, 512)])
+    add("V", lambda: V.memset(T.tiny[:], -TINY), [], [R("tiny")])
+    add("V", lambda: V.tensor_scalar(T.pi[:, 1:2], T.pi[:, 0:1], 3, None, ALU.bitwise_and), [R("pi", 0, 1)], [R("pi", 1, 2)])
+    add("V", lambda: V.tensor_scalar(T.pi[:, 2:3], T.pi[:, 0:1], 2, 3, ALU.logical_shift_right, ALU.bitwise_and),
+        [R("pi", 0, 1)], [R("pi", 2, 3)])
+    add("V", lambda: V.tensor_copy(T.pf[:, 1:3], T.pi[:, 1:3]), [R("pi", 1, 3)], [R("pf", 1, 3)])
     add("V", lambda: V.tensor_scalar(T.band[:, 3:515:4], T.jp[:], 0.0, None, ALU.is_equal), [R("jp")], [R("band")])
-    add("V", lambda: V.memset(T.neg[:], LOW), [], [R("neg")])
-    add("V", lambda: V.tensor_copy(T.uo16[:], T.uo32[:]), [R("uo32")], [R("uo16")])
+    add("V", lambda: V.tensor_copy(T.l16[:, 0:8], T.lf[:, 0:8]), [R("lf", 0, 8)], [R("l16", 0, 8)])
+    add("V", lambda: V.tensor_scalar(T.pf[:, 3:4], T.pf[:, 1:2], 32.0, T.pf[:, 2:3], ALU.mult, ALU.add),
+        [R("pf", 1, 3)], [R("pf", 3, 4)])
     for b in range(4):
         quant("qe", "se", 128 * b, 128 * b + 128, T.band[:, 3 - b:515 - b], [R("band")])
+    add("V", lambda: V.tensor_scalar(T.l16[:, 8:24], T.lf[:, 8:24], T.pf[:, 2:3], None, ALU.add),
+        [R("lf", 8, 24), R("pf", 2, 3)], [R("l16", 8, 24)])
+    add("V", lambda: V.tensor_scalar(T.l16[:, 24:40], T.lf[:, 24:40], T.pf[:, 3:4], None, ALU.add),
+        [R("lf", 24, 40), R("pf", 3, 4)], [R("l16", 24, 40)])
 
     quant("qu", "su", 0, 128, T.us[:], [R("us")])
-    quant_z(0)
-    add("V", lambda: V.tensor_copy(T.qur[:].bitcast(dt.uint32), T.qu[:].bitcast(dt.uint32).indirect(T.uo16[:])),
-        [R("qu"), R("uo16")], [R("qur")])
-    add("S", lambda: S.activation(T.sur[:], T.su[:].indirect(T.uo16[:]), ACT.Copy), [R("su"), R("uo16")], [R("sur")])
-    mm(5, "qur", "sur", 0, "qz0", "sz0", 0, 128)
-    quant_x(0, HALF, C)
+    add("V", lambda: V.tensor_scalar(T.c4[:, 0:44], T.cc[:], 4.0, None, ALU.mult), [R("cc")], [R("c4", 0, 44)])
+    add("S", lambda: S.activation(T.sur[:], T.su[:].indirect(T.l16[:, 0:8]), ACT.Copy), [R("su"), R("l16", 0, 8)], [R("sur")])
     add("V", lambda: V.tensor_copy(T.co16[:], T.cc[:, 0:20]), [R("cc")], [R("co16")])
-    add("V", lambda: V.tensor_copy(T.ccf[:], T.cc[:]), [R("cc")], [R("ccf")])
+    add("V", lambda: V.transpose(T.c4t[:], T.c4[:]), [R("c4")], [R("c4t")])
+    add("V", lambda: V.tensor_copy(T.qur[:].bitcast(dt.uint32), T.qu[:].bitcast(dt.uint32).indirect(T.l16[:, 0:8])),
+        [R("qu"), R("l16", 0, 8)], [R("qur")])
+    add("S", lambda: S.activation(T.c4h[:], T.c4t[:].indirect(T.l16[:, 8:24]), ACT.Copy), [R("c4t"), R("l16", 8, 24)], [R("c4h")])
     add("S", lambda: S.activation(T.coord[:], T.ramp[:].indirect(T.co16[:]), ACT.Copy), [R("ramp"), R("co16")], [R("coord")])
+    quant_x(0, HALF, C)
     mm(4, "qur", "sur", 0, "qx0", "sx0", HALF, C)
-    sign(0)
+    add("V", lambda: V.transpose(T.c4u[:], T.c4h[:]), [R("c4h")], [R("c4u")])
+    add("S", lambda: S.activation(T.tab[:], T.c4u[:].indirect(T.l16[:, 24:35]), ACT.Copy), [R("c4u"), R("l16", 24, 40)], [R("tab")])
+
+    scan(0, 1, 4)
     quant_x(0, 0, HALF)
     mm(6, "qur", "sur", 0, "qx0", "sx0", 0, HALF)
-    sign_scaled(0, 2, -1.0)
-    scan(0, 1, 4)
     count(0, 1)
+    peak1(0)
     scan(0, 0, 6)
     count(0, 0)
-    peak1(0, "V")
     higher(0)
+    quant("qz0", "sz0", 0, 128, T.bt0[:, 0:4 * TL], [R("bt0", 0, TL)])
+    mm(5, "qur", "sur", 0, "qz0", "sz0", 0, 128)
     peaks16(0)
     peak_coords(0)
-    dist_tail(0)
-    offs_tail(0)
-    dist_own(0, 0)
-    dist_own(0, 1)
+    for e in range(3):
+        dist(0, e)
+    sign(0)
+    offsets(0)
 
     sent = 0
     for t in range(ROUNDS):
         last = t == ROUNDS - 1
         qn, sn = "qx%d" % (t + 1), "sx%d" % (t + 1)
         store_peaks(t)
-        for b in (2, 0, 3, 1):
-            tail(t, b)
+        gather(t, "V", "gt%d" % t, 0, CUT, 0)
+        gather(t, "S", "gt%d" % t, CUT, TL, 0)
         quant("qg%d" % t, "sg%d" % t, 0, TL, T["gt%d" % t][:], [R("gt%d" % t)])
         sent += send(t)
         src = T.cores[(rank - STEP[t]) % n_ranks]
         landed = 2 * len(topo.engines(src, core))
-        add("V", lambda t=t: V.tensor_copy(T["ofe%d" % t][:], T["abe%d" % t][:]), [R("abe%d" % t)], [R("ofe%d" % t)])
-        if t > 0:
-            sign_scaled(t, 2, -1.0)
-        for b in range(4):
-            window(t, b)
-        if not last:
-            if t == 0:
-                add("S", lambda: S.activation(T.aux0[:], T.bms[:], ACT.Copy, scale=32.0), [R("bms")], [R("aux0")])
-            else:
-                add("S", lambda t=t: S.activation(T["aux%d" % t][:], T["bp%d" % t][:], ACT.Copy, scale=0.5),
-                    [R("bp%d" % t)], [R("aux%d" % t)])
-            add("S", lambda t=t: S.activation(T.hcol[:, 4 * t:4 * t + 4], T.z[:, 0:4], ACT.Copy, scale=0.5),
-                [R("z", 0, 4)], [R("hcol", 4 * t, 4 * t + 4)])
-        for b in range(4):
-            subtract(t, b, False)
+        for a, b in [(LATE, TL)] + EARLY:
+            gather(t, "S", "ge%d" % t, a, b, NT)
+        if last:
+            quant("qv", "sv", 0, 128, T.vs[:], [R("vs")])
+        gather(t, "V", "ge%d" % t, 0, LATE, NT)
+        subtract(t, 0, TL)
+        for a, b in EARLY:
+            subtract(t, a, b)
         quant_x(t + 1, TL, C)
         if not last:
-            mm(0, "qur", "sur", 0, qn, sn, HALF, C)
-            for b in range(4):
-                mm(4 + b, "wq", "wsc", 128 * b, qn, sn, TL, C)
-        else:
+            halve(t, TL, C)
+            col0 = T.bt0 if t == 0 else T.z
+            add("S", lambda t=t, col0=col0: S.activation(T.hcol[:, 4 * t:4 * t + 4], col0[:, 0:4], ACT.Copy, scale=0.5),
+                [R("z", 0, 4), R("bt0")], [R("hcol", 4 * t, 4 * t + 4)])
+            halve(t, 0, TL)
+        for b in range(4):
+            mm(b, "qe", "se", 128 * b, "lq%d" % t, "ls%d" % t, 0, TL, ext=[("arr%d" % t, landed)] if b == 0 else [])
+        if last:
             add("Y", lambda: Y.dma_start(T.oc[:, 4 * TL:4 * C], T[qn][:, TL:C].bitcast(dt.uint8)), [R(qn, TL, C)], [], sem="sty")
-            quant("qv", "sv", 0, 128, T.vs[:], [R("vs")])
             mm(4, "qv", "sv", 0, qn, sn, TL, C)
             add("S", lambda: S.activation(T.ysb[:, TL:C], T.ps[:, 512 * 4:512 * 4 + C - TL], ACT.Copy),
                 [bank(4)], [R("ysb", TL, C)])
             add("Y", lambda: Y.dma_start(T.y[:, TL:C], T.ysb[:, TL:C]), [R("ysb", TL, C)], [], sem="sty")
+        else:
+            mm(4, "qur", "sur", 0, qn, sn, HALF, C)
+            layer(t, 0, False)
+            layer(t, 1, False)
         for b in range(4):
-            subtract(t, b, True)
-        if not last:
-            scan(t + 1, 1, 0)
-            count(t + 1, 1)
-            peak1(t + 1, "S")
-            for b in range(3):
-                beam(t, b, False)
-        order = (1, 2, 3, 0)
-        for b in order:
-            mm(b, "qe", "se", 128 * b, "lq%d" % t, "ls%d" % t, 0, TL,
-               ext=[("arr%d" % t, landed)] if b == order[0] else [])
-        for b in order:
             arrived(t, b)
         quant_x(t + 1, 0, TL)
         if last:
             break
         if t == 0:
-            add("Y", lambda: Y.dma_start(T.vs[:], T.v[:]), [R("xs1", 0, TL, order[0])], [R("vs")], sem="lv")
-        mm(4, "qur", "sur", 0, qn, sn, 0, HALF)
+            add("Y", lambda: Y.dma_start(T.vs[:], T.v[:]), [R("xs1", 0, TL, 0)], [R("vs")], sem="lv")
+        mm(7, "qur", "sur", 0, qn, sn, 0, HALF)
         for b in range(4):
-            mm(b, "wq", "wsc", 128 * b, qn, sn, 0, TL)
-        beam(t, 3, False)
-        scan(t + 1, 0, 4)
+            layer(t, b, True)
+        scan(t + 1, 1, 4)
+        count(t + 1, 1)
+        peak1(t + 1)
+        beam(t, 0, False)
+        layer(t, 2, False)
+        scan(t + 1, 0, 7)
+        layer(t, 3, False)
         beam_col0(t, 0)
         beam_col0(t, 1)
         count(t + 1, 0)
+        higher(t + 1)
+        beam(t, 1, False)
+        beam(t, 0, True)
         beam_col0(t, 2)
         beam_col0(t, 3)
-        higher(t + 1)
-        beam(t, 0, True)
-        beam(t, 1, True)
         peaks16(t + 1)
-        quant_z(t + 1)
+        beam(t, 1, True)
+        quant("qz%d" % (t + 1), "sz%d" % (t + 1), 0, 128, T.z[:], [R("z")])
         mm(5, "qur", "sur", 0, "qz%d" % (t + 1), "sz%d" % (t + 1), 0, 128)
         peak_coords(t + 1)
         beam(t, 2, True)
         beam(t, 3, True)
-        dist_tail(t + 1)
-        dist_own(t + 1, 0)
-        dist_own(t + 1, 1)
+        beam(t, 2, False)
+        beam(t, 3, False)
+        for e in range(3):
+            dist(t + 1, e)
         sign(t + 1)
-        offs_tail(t + 1)
-        sign_scaled(t + 1, 1, 1.0)
+        offsets(t + 1)
 
     qn, sn = "qx%d" % ROUNDS, "sx%d" % ROUNDS
     mm(5, "qv", "sv", 0, qn, sn, 0, TL)

@@ -4,9 +4,9 @@ ALU = AluOpType
 ACT = ActivationFunctionType
 C, TL, ROUNDS = 320, 128, 3
 HALF = C // 2
-CUT = 72
-LATE = 48
-EARLY = [(128, 224), (224, 320)]
+CUT = 64
+OWN = [(40, 104), (40, 104), (24, 96)]
+EARLY = [(128, 256), (256, 320)]
 EARLY_BANK = [5, 6, 4, 7]
 STEP = [1, 2, 1]
 LOW = -9.0e29
@@ -29,7 +29,7 @@ SCRATCH = {
     "tab": ("sbuf", [128, 176], "float32"),
     "pi": ("sbuf", [128, 4], "int32"), "pf": ("sbuf", [128, 4], "float32"),
     "lf": ("sbuf", [128, 40], "float32"), "l16": ("sbuf", [128, 40], "uint16"),
-    "jp": ("sbuf", [128, 128], "bfloat16"), "band": ("sbuf", [128, 520], "bfloat16"),
+    "row": ("sbuf", [128, 4], "float32"), "band": ("sbuf", [128, 520], "bfloat16"),
     "ramp": ("sbuf", [128, C], "float32"), "coord": ("sbuf", [128, C], "float32"),
     "nil": ("sbuf", [128, HALF], "float32"), "tiny": ("sbuf", [128, 4], "float32"),
     "z": ("sbuf", [128, 512], "bfloat16"),
@@ -200,15 +200,14 @@ def rank_program(g, core, T, topo):
             [R("yk%d" % t, 3, 4), R("ramp")], [R("yk%d" % t, 2, 3)])
 
     def higher(t):
-        run, yk = T["run%d" % t], T["yk%d" % t]
-        add("V", lambda: V.tensor_scalar(yk[:, 0:1], run[:, HALF - 1:HALF], run[:, C - 1:C], yk[:, 2:3],
-                                         ALU.is_lt, ALU.mult),
-            [R("run%d" % t), R("yk%d" % t, 2, 3)], [R("yk%d" % t, 0, 1)])
+        run = T["run%d" % t]
+        add("S", lambda: S.activation(T.row[:, 0:1], run[:, HALF - 1:HALF], ACT.Sign, bias=run[:, C - 1:C], scale=-1.0),
+            [R("run%d" % t)], [R("row", 0, 1)])
 
     def peaks16(t):
         yk, kk = T["yk%d" % t], T["kk%d" % t]
-        add("V", lambda: V.tensor_scalar(kk[:, 0:3], yk[:, 0:3], yk[:, 1:2], None, ALU.max),
-            [R("yk%d" % t, 0, 3)], [R("kk%d" % t)])
+        add("V", lambda: V.tensor_scalar(kk[:, 0:3], T.row[:, 0:3], yk[:, 2:3], yk[:, 1:2], ALU.mult, ALU.max),
+            [R("yk%d" % t, 1, 3), R("row")], [R("kk%d" % t)])
 
     def store_peaks(t):
         yk = T["yk%d" % t]
@@ -224,9 +223,12 @@ def rank_program(g, core, T, topo):
                                       bias=T["na%d" % t][:, 16 * e:16 * e + 1]),
             [R("tab"), R("na%d" % t)], [R("ab%d" % t, to, to + n)])
 
-    def offsets(t):
-        add("V", lambda: V.tensor_scalar(T["of%d" % t][:], T["ab%d" % t][:], T.pf[:, 1:2], None, ALU.add),
-            [R("ab%d" % t), R("pf")], [R("of%d" % t)])
+    def offsets(t, a, b):
+        add("V", lambda: V.tensor_scalar(T["of%d" % t][:, a:b], T["ab%d" % t][:, a:b], T.pf[:, 1:2], None, ALU.add),
+            [R("ab%d" % t, a, b), R("pf")], [R("of%d" % t, a, b)])
+
+    def unit(b):
+        quant("qe", "se", 128 * b, 128 * b + 128, T.band[:, 3 - b:515 - b], [R("band")])
 
     def size(t):
         return 1.0 if t == 0 else 0.015625
@@ -294,9 +296,9 @@ def rank_program(g, core, T, topo):
                                       bias=T.hcol[:, 4 * t + b:4 * t + b + 1], scale=0.015625),
             [bank(b), R("hcol", 4 * t, 4 * t + 4)], [R("z", b, b + 1)])
 
+    add("Y", lambda: Y.dma_start(T.cc[:, 0:20], T.co[:]), [], [R("cc", 0, 20)], sem="lcc")
+    add("Y", lambda: Y.dma_start(T.cc[:, 20:44], T.cn[:]), [], [R("cc", 20, 44)], sem="lcc")
     add("Y", lambda: Y.dma_start(T.us[:], T.u[:]), [], [R("us")], sem="lu")
-    add("S", lambda: S.dma_start(T.cc[:, 0:20], T.co[:]), [], [R("cc", 0, 20)], sem="lcc")
-    add("S", lambda: S.dma_start(T.cc[:, 20:44], T.cn[:]), [], [R("cc", 20, 44)], sem="lcc")
     add("Y", lambda: Y.dma_start(T.xs0[:, 4 * HALF:4 * C], T.x[:, 4 * HALF:4 * C]), [], [R("xs0", HALF, C)], sem="lx1")
     add("Y", lambda: Y.dma_start(T.xs0[:, 0:4 * HALF], T.x[:, 0:4 * HALF]), [], [R("xs0", 0, HALF)], sem="lx0")
     add("Y", lambda: Y.dma_start(T.bt0[:, 0:4 * TL], T.bm[:, 0:4 * TL]), [], [R("bt0", 0, TL)], sem="lb0")
@@ -305,61 +307,62 @@ def rank_program(g, core, T, topo):
     add("Y", lambda: Y.dma_start(T.wsc[:], T.ws[:]), [], [R("wsc")], sem="lw")
 
     iota("pi", 0, 1, [[0, 1]], 1, whole=True)
-    iota("jp", 0, 128, [[1, 128]], -1)
-    iota("lf", 0, 8, [[16, 8]], 0)
     iota("lf", 8, 24, [[32, 2], [4, 4], [16, 2]], 0)
-    iota("c4", 44, 64, [[0, 20]], 0)
+    iota("lf", 0, 8, [[16, 8]], 0)
     iota("lf", 24, 40, [[128, 2], [4, 8]], 0)
     iota("ramp", 0, C, [[1, C]], 0)
     iota("nil", 0, HALF, [[0, HALF]], 0)
+    iota("row", 1, 3, [[1, 2]], 0)
     iota("z", 4, 512, [[0, 508]], 0)
     add("V", lambda: V.memset(T.band[:], 0.0), [], [R("band")])
+    add("V", lambda: V.memset(T.c4[:, 44:64], 0.0), [], [R("c4", 44, 64)])
     add("V", lambda: V.memset(T.tiny[:], -TINY), [], [R("tiny")])
     add("V", lambda: V.tensor_scalar(T.pi[:, 1:2], T.pi[:, 0:1], 3, None, ALU.bitwise_and), [R("pi", 0, 1)], [R("pi", 1, 2)])
     add("V", lambda: V.tensor_scalar(T.pi[:, 2:3], T.pi[:, 0:1], 2, 3, ALU.logical_shift_right, ALU.bitwise_and),
         [R("pi", 0, 1)], [R("pi", 2, 3)])
-    add("V", lambda: V.tensor_copy(T.pf[:, 1:3], T.pi[:, 1:3]), [R("pi", 1, 3)], [R("pf", 1, 3)])
-    add("V", lambda: V.tensor_scalar(T.band[:, 3:515:4], T.jp[:], 0.0, None, ALU.is_equal), [R("jp")], [R("band")])
-    add("V", lambda: V.tensor_copy(T.l16[:, 0:8], T.lf[:, 0:8]), [R("lf", 0, 8)], [R("l16", 0, 8)])
-    add("V", lambda: V.tensor_scalar(T.pf[:, 3:4], T.pf[:, 1:2], 32.0, T.pf[:, 2:3], ALU.mult, ALU.add),
-        [R("pf", 1, 3)], [R("pf", 3, 4)])
-    for b in range(4):
-        quant("qe", "se", 128 * b, 128 * b + 128, T.band[:, 3 - b:515 - b], [R("band")])
+    add("V", lambda: V.tensor_copy(T.pf[:, 0:3], T.pi[:, 0:3]), [R("pi", 0, 3)], [R("pf", 0, 3)])
     add("V", lambda: V.tensor_scalar(T.l16[:, 8:24], T.lf[:, 8:24], T.pf[:, 2:3], None, ALU.add),
         [R("lf", 8, 24), R("pf", 2, 3)], [R("l16", 8, 24)])
+    add("V", lambda: V.tensor_scalar(T.pf[:, 3:4], T.pf[:, 1:2], 32.0, T.pf[:, 2:3], ALU.mult, ALU.add),
+        [R("pf", 1, 3)], [R("pf", 3, 4)])
+    add("V", lambda: V.tensor_copy(T.l16[:, 0:8], T.lf[:, 0:8]), [R("lf", 0, 8)], [R("l16", 0, 8)])
     add("V", lambda: V.tensor_scalar(T.l16[:, 24:40], T.lf[:, 24:40], T.pf[:, 3:4], None, ALU.add),
         [R("lf", 24, 40), R("pf", 3, 4)], [R("l16", 24, 40)])
 
-    quant("qu", "su", 0, 128, T.us[:], [R("us")])
     add("V", lambda: V.tensor_scalar(T.c4[:, 0:44], T.cc[:], 4.0, None, ALU.mult), [R("cc")], [R("c4", 0, 44)])
-    add("S", lambda: S.activation(T.sur[:], T.su[:].indirect(T.l16[:, 0:8]), ACT.Copy), [R("su"), R("l16", 0, 8)], [R("sur")])
     add("V", lambda: V.tensor_copy(T.co16[:], T.cc[:, 0:20]), [R("cc")], [R("co16")])
     add("V", lambda: V.transpose(T.c4t[:], T.c4[:]), [R("c4")], [R("c4t")])
+    add("S", lambda: S.activation(T.c4h[:], T.c4t[:].indirect(T.l16[:, 8:24]), ACT.Copy), [R("c4t"), R("l16", 8, 24)], [R("c4h")])
+    quant("qu", "su", 0, 128, T.us[:], [R("us")])
+    add("S", lambda: S.activation(T.sur[:], T.su[:].indirect(T.l16[:, 0:8]), ACT.Copy), [R("su"), R("l16", 0, 8)], [R("sur")])
+    add("S", lambda: S.activation(T.coord[:], T.ramp[:].indirect(T.co16[:]), ACT.Copy), [R("ramp"), R("co16")], [R("coord")])
     add("V", lambda: V.tensor_copy(T.qur[:].bitcast(dt.uint32), T.qu[:].bitcast(dt.uint32).indirect(T.l16[:, 0:8])),
         [R("qu"), R("l16", 0, 8)], [R("qur")])
-    add("S", lambda: S.activation(T.c4h[:], T.c4t[:].indirect(T.l16[:, 8:24]), ACT.Copy), [R("c4t"), R("l16", 8, 24)], [R("c4h")])
-    add("S", lambda: S.activation(T.coord[:], T.ramp[:].indirect(T.co16[:]), ACT.Copy), [R("ramp"), R("co16")], [R("coord")])
     quant_x(0, HALF, C)
     mm(4, "qur", "sur", 0, "qx0", "sx0", HALF, C)
     add("V", lambda: V.transpose(T.c4u[:], T.c4h[:]), [R("c4h")], [R("c4u")])
-    add("S", lambda: S.activation(T.tab[:], T.c4u[:].indirect(T.l16[:, 24:35]), ACT.Copy), [R("c4u"), R("l16", 24, 40)], [R("tab")])
-
-    scan(0, 1, 4)
     quant_x(0, 0, HALF)
     mm(6, "qur", "sur", 0, "qx0", "sx0", 0, HALF)
+    scan(0, 1, 4)
+    add("S", lambda: S.activation(T.tab[:], T.c4u[:].indirect(T.l16[:, 24:35]), ACT.Copy), [R("c4u"), R("l16", 24, 40)], [R("tab")])
     count(0, 1)
-    peak1(0)
     scan(0, 0, 6)
     count(0, 0)
+    peak1(0)
     higher(0)
     quant("qz0", "sz0", 0, 128, T.bt0[:, 0:4 * TL], [R("bt0", 0, TL)])
     mm(5, "qur", "sur", 0, "qz0", "sz0", 0, 128)
+    add("V", lambda: V.tensor_scalar(T.band[:, 3:515:4], T.ramp[:, 0:128], T.pf[:, 0:1], None, ALU.is_equal),
+        [R("ramp"), R("pf", 0, 1)], [R("band")])
+    unit(0)
     peaks16(0)
+    sign(0)
     peak_coords(0)
+    unit(1)
+    unit(2)
     for e in range(3):
         dist(0, e)
-    sign(0)
-    offsets(0)
+    offsets(0, 0, NT)
 
     sent = 0
     for t in range(ROUNDS):
@@ -368,19 +371,23 @@ def rank_program(g, core, T, topo):
         store_peaks(t)
         gather(t, "V", "gt%d" % t, 0, CUT, 0)
         gather(t, "S", "gt%d" % t, CUT, TL, 0)
+        if t == 0:
+            offsets(0, NT, NT + NO)
         quant("qg%d" % t, "sg%d" % t, 0, TL, T["gt%d" % t][:], [R("gt%d" % t)])
         sent += send(t)
         src = T.cores[(rank - STEP[t]) % n_ranks]
         landed = 2 * len(topo.engines(src, core))
-        for a, b in [(LATE, TL)] + EARLY:
+        own, cut = OWN[t]
+        for a, b in [(own, cut)] + EARLY + [(cut, TL)]:
             gather(t, "S", "ge%d" % t, a, b, NT)
         if last:
             quant("qv", "sv", 0, 128, T.vs[:], [R("vs")])
-        gather(t, "V", "ge%d" % t, 0, LATE, NT)
-        subtract(t, 0, TL)
-        for a, b in EARLY:
+        gather(t, "V", "ge%d" % t, 0, own, NT)
+        for a, b in [(0, cut)] + EARLY + [(cut, TL)]:
             subtract(t, a, b)
         quant_x(t + 1, TL, C)
+        if t == 0:
+            unit(3)
         if not last:
             halve(t, TL, C)
             col0 = T.bt0 if t == 0 else T.z
@@ -422,21 +429,22 @@ def rank_program(g, core, T, topo):
         higher(t + 1)
         beam(t, 1, False)
         beam(t, 0, True)
+        beam(t, 1, True)
         beam_col0(t, 2)
         beam_col0(t, 3)
         peaks16(t + 1)
-        beam(t, 1, True)
+        beam(t, 2, True)
         quant("qz%d" % (t + 1), "sz%d" % (t + 1), 0, 128, T.z[:], [R("z")])
         mm(5, "qur", "sur", 0, "qz%d" % (t + 1), "sz%d" % (t + 1), 0, 128)
         peak_coords(t + 1)
-        beam(t, 2, True)
         beam(t, 3, True)
         beam(t, 2, False)
-        beam(t, 3, False)
         for e in range(3):
             dist(t + 1, e)
         sign(t + 1)
-        offsets(t + 1)
+        offsets(t + 1, 0, NT)
+        beam(t, 3, False)
+        offsets(t + 1, NT, NT + NO)
 
     qn, sn = "qx%d" % ROUNDS, "sx%d" % ROUNDS
     mm(5, "qv", "sv", 0, qn, sn, 0, TL)

from concourse.mybir import dt, AluOpType, ActivationFunctionType

ALU = AluOpType
ACT = ActivationFunctionType
C, TL, ROUNDS = 320, 128, 3
HALF = C // 2
CUT = 64
OWN = [(40, 104), (40, 104), (24, 96)]
EARLY = [(128, 256), (256, 320)]
EARLY_BANK = [5, 6, 4, 7]
STEP = [1, 2, 1]
LOW = -9.0e29
TINY = 2.0 ** -120
CODES, PLANE = "float8_e4m3fn_x4", "uint8"
NO, NT = C // 4, TL // 4

SCRATCH = {
    "bt0": ("sbuf", [128, 4 * C], "bfloat16"),
    "us": ("sbuf", [128, 512], "bfloat16"),
    "vs": ("sbuf", [128, 512], "bfloat16"),
    "qu": ("sbuf", [128, 128], CODES), "su": ("sbuf", [128, 128], PLANE),
    "qur": ("sbuf", [128, 128], CODES), "sur": ("sbuf", [128, 128], PLANE),
    "qv": ("sbuf", [128, 128], CODES), "sv": ("sbuf", [128, 128], PLANE),
    "wq": ("sbuf", [128, 512], CODES), "wsc": ("sbuf", [128, 512], PLANE),
    "qe": ("sbuf", [128, 512], CODES), "se": ("sbuf", [128, 512], PLANE),
    "cc": ("sbuf", [128, 44], "int32"), "co16": ("sbuf", [128, 20], "uint16"),
    "c4": ("sbuf", [128, 64], "float32"), "c4t": ("sbuf", [128, 64], "float32"),
    "c4h": ("sbuf", [128, 256], "float32"), "c4u": ("sbuf", [128, 256], "float32"),
    "tab": ("sbuf", [128, 176], "float32"),
    "pi": ("sbuf", [128, 4], "int32"), "pf": ("sbuf", [128, 4], "float32"),
    "lf": ("sbuf", [128, 40], "float32"), "l16": ("sbuf", [128, 40], "uint16"),
    "row": ("sbuf", [128, 4], "float32"), "band": ("sbuf", [128, 520], "bfloat16"),
    "ramp": ("sbuf", [128, C], "float32"), "coord": ("sbuf", [128, C], "float32"),
    "nil": ("sbuf", [128, HALF], "float32"), "tiny": ("sbuf", [128, 4], "float32"),
    "z": ("sbuf", [128, 512], "bfloat16"),
    "hcol": ("sbuf", [128, 8], "float32"),
    "junk": ("sbuf", [128, C], "float32"),
    "ysb": ("sbuf", [128, C], "float32"),
    "ps": ("psum", [128, 4096], "float32"),
}
for _t in range(ROUNDS + 1):
    SCRATCH["xs%d" % _t] = ("sbuf", [128, 4 * C], "bfloat16")
    SCRATCH["qx%d" % _t] = ("sbuf", [128, C], CODES)
    SCRATCH["sx%d" % _t] = ("sbuf", [128, C], PLANE)
for _t in range(ROUNDS):
    SCRATCH["run%d" % _t] = ("sbuf", [128, C], "float32")
    SCRATCH["yk%d" % _t] = ("sbuf", [128, 4], "float32")
    SCRATCH["kk%d" % _t] = ("sbuf", [128, 4], "uint16")
    SCRATCH["na%d" % _t] = ("sbuf", [128, 48], "float32")
    SCRATCH["ab%d" % _t] = ("sbuf", [128, NT + NO], "float32")
    SCRATCH["of%d" % _t] = ("sbuf", [128, NT + NO], "uint16")
    SCRATCH["cs%d" % _t] = ("sbuf", [128, 4], "float32")
    SCRATCH["ge%d" % _t] = ("sbuf", [128, 4 * C], "bfloat16")
    SCRATCH["gt%d" % _t] = ("sbuf", [128, 4 * TL], "bfloat16")
    SCRATCH["qg%d" % _t] = ("sbuf", [128, TL], CODES)
    SCRATCH["sg%d" % _t] = ("sbuf", [128, TL], PLANE)
    SCRATCH["lq%d" % _t] = ("sbuf", [128, TL], CODES)
    SCRATCH["ls%d" % _t] = ("sbuf", [128, TL], PLANE)
    SCRATCH["qz%d" % _t] = ("sbuf", [128, 128], CODES)
    SCRATCH["sz%d" % _t] = ("sbuf", [128, 128], PLANE)
    SCRATCH["el%d" % _t] = ("sbuf", [128, 4 * TL], "float32")
for _t in range(ROUNDS - 1):
    SCRATCH["aux%d" % _t] = ("sbuf", [128, 4 * C], "bfloat16")
    SCRATCH["bt%d" % (_t + 1)] = ("sbuf", [128, 4 * C], "bfloat16")

SEMAPHORES = ["cv", "cs", "cp", "cg", "lu", "lx0", "lx1", "lb0", "lb1", "lcc", "lw", "lv",
              "sty", "sts", "arr0", "arr1", "arr2", "loc"]
COUNTER = {"V": "cv", "S": "cs", "P": "cp", "G": "cg"}


def R(name, lo=0, hi=1 << 20, plane=None):
    return (name, lo, hi, plane)


def bank(k):
    return ("ps", k, k + 1, None)


def meets(a, b):
    return a[0] == b[0] and a[1] < b[2] and b[1] < a[2] and (a[3] is None or b[3] is None or a[3] == b[3])


def clash(a, b):
    for w in a["w"]:
        for r in b["r"] + b["w"]:
            if meets(w, r):
                return True
    for r in a["r"]:
        for w in b["w"]:
            if meets(r, w):
                return True
        if r[0] == "ps" and a["q"] != b["q"]:
            for r2 in b["r"]:
                if meets(r, r2):
                    return True
    return False


def emit(g, T, ops, ends):
    queue = {"V": g.vector, "S": g.scalar, "P": g.tensor, "G": g, "Y": g.sync}
    known = {q: {} for q in queue}
    place = {q: 0 for q in queue}
    total = {}
    for n, op in enumerate(ops):
        q = op["q"]
        need = {}
        for a in ops[:n]:
            if clash(a, op):
                key = a["key"]
                if known[q].get(key, 0) < a["pos"] and (key not in need or need[key]["pos"] < a["pos"]):
                    need[key] = a
        waits = []
        for a in sorted(need.values(), key=lambda e: -e["n"]):
            if known[q].get(a["key"], 0) >= a["pos"]:
                continue
            waits.append(a)
            a["mark"] = True
            for k, v in a["seen"].items():
                if known[q].get(k, 0) < v:
                    known[q][k] = v
            known[q][a["key"]] = total[a["key"]] if a["sem"] else a["pos"]
        op["waits"] = [(a, total[a["key"]] if a["sem"] else None) for a in waits]
        op["seen"] = dict(known[q])
        op["n"] = n
        if op["sem"]:
            op["key"] = op["sem"]
            total[op["key"]] = total.get(op["key"], 0) + 16
            op["pos"] = total[op["key"]]
        else:
            op["key"] = q
            place[q] += 1
            op["pos"] = place[q]
    count = {q: 0 for q in queue}
    for op in ops:
        if op.get("mark") and not op["sem"]:
            count[op["q"]] += 1
            op["count"] = count[op["q"]]
    for op in ops:
        e = queue[op["q"]]
        for sem, val in op["ext"]:
            e.wait_ge(T.sem[sem], val)
        for a, val in op["waits"]:
            if a["sem"]:
                e.wait_ge(T.sem[a["sem"]], val)
            else:
                e.wait_ge(T.sem[COUNTER[a["q"]]], a["count"])
        ins = op["f"]()
        if op["sem"]:
            ins.then_inc(T.sem[op["sem"]], 16)
        elif op.get("mark"):
            ins.then_inc(T.sem[COUNTER[op["q"]]], 1)
    for q, sem, val in ends:
        queue[q].wait_ge(T.sem[sem], total[sem] if val is None else val)


def rank_program(g, core, T, topo):
    rank = T.rank_of(core)
    if rank is None:
        return
    n_ranks = len(T.cores)
    V, S, P, Y = g.vector, g.scalar, g.tensor, g.sync
    ops = []

    def add(q, f, r, w, sem=None, ext=()):
        ops.append({"q": q, "f": f, "r": list(r), "w": list(w), "sem": sem, "ext": list(ext)})

    def quant(codes, scales, a, b, view, rd):
        add("V", lambda: V.quantize_mx(T[codes][:, a:b], T[scales][:, a:b], view),
            rd, [R(codes, a, b), R(scales, a, b)])

    def mm(k, lq, ls, la, rq, rs, a, b, ext=()):
        add("P", lambda: P.matmul_mx(T.ps[:, 512 * k:512 * k + b - a], T[lq][:, la:la + 128], T[ls][:, la:la + 128],
                                     T[rq][:, a:b], T[rs][:, a:b], True, True),
            [R(lq, la, la + 128), R(ls, la, la + 128), R(rq, a, b), R(rs, a, b)], [bank(k)], ext=ext)

    def iota(name, a, b, pattern, per_partition, whole=False):
        flag = {} if whole else {"allow_small_or_imprecise_dtypes": True}
        add("G", lambda: g.iota(T[name][:, a:b], pattern, 0, per_partition, **flag), [], [R(name, a, b)])

    def quant_x(t, a, b):
        quant("qx%d" % t, "sx%d" % t, a, b, T["xs%d" % t][:, 4 * a:4 * b], [R("xs%d" % t, a, b)])

    def scan(t, f, k):
        run = T["run%d" % t]
        add("V", lambda: V.tensor_tensor_scan(run[:, HALF * f:HALF * f + HALF], T.ps[:, 512 * k:512 * k + HALF],
                                              T.nil[:], LOW, ALU.max, ALU.add),
            [bank(k), R("nil")], [R("run%d" % t, HALF * f, HALF * f + HALF)])

    def count(t, f):
        run, yk = T["run%d" % t], T["yk%d" % t]
        col = 1 if f == 0 else 3
        a, b = HALF * f, HALF * f + HALF
        add("S", lambda: S.activation(T.junk[:, a:b], run[:, a:b], ACT.Sign, bias=run[:, b - 1:b], scale=-1.0,
                                      accum_out=yk[:, col:col + 1]),
            [R("run%d" % t, a, b)], [R("junk", a, b), R("yk%d" % t, col, col + 1)])

    def peak1(t):
        yk = T["yk%d" % t]
        add("S", lambda: S.activation(yk[:, 2:3], yk[:, 3:4], ACT.Identity, bias=T.ramp[:, HALF:HALF + 1]),
            [R("yk%d" % t, 3, 4), R("ramp")], [R("yk%d" % t, 2, 3)])

    def higher(t):
        run = T["run%d" % t]
        add("S", lambda: S.activation(T.row[:, 0:1], run[:, HALF - 1:HALF], ACT.Sign, bias=run[:, C - 1:C], scale=-1.0),
            [R("run%d" % t)], [R("row", 0, 1)])

    def peaks16(t):
        yk, kk = T["yk%d" % t], T["kk%d" % t]
        add("V", lambda: V.tensor_scalar(kk[:, 0:3], T.row[:, 0:3], yk[:, 2:3], yk[:, 1:2], ALU.mult, ALU.max),
            [R("yk%d" % t, 1, 3), R("row")], [R("kk%d" % t)])

    def store_peaks(t):
        yk = T["yk%d" % t]
        add("Y", lambda: Y.dma_start(T.ol[:, 2 * t:2 * t + 2], yk[0:128:16, 1:3]), [R("yk%d" % t, 1, 3)], [], sem="sty")

    def peak_coords(t):
        add("S", lambda: S.activation(T["na%d" % t][:], T.coord[:].indirect(T["kk%d" % t][:, 0:3]), ACT.Copy, scale=-4.0),
            [R("coord"), R("kk%d" % t)], [R("na%d" % t)])

    def dist(t, e):
        a, n, to = [(NO + NT * t, NT, 0), (0, NO // 2, NT), (NO // 2, NO // 2, NT + NO // 2)][e]
        add("S", lambda: S.activation(T["ab%d" % t][:, to:to + n], T.tab[:, a:a + n], ACT.Abs,
                                      bias=T["na%d" % t][:, 16 * e:16 * e + 1]),
            [R("tab"), R("na%d" % t)], [R("ab%d" % t, to, to + n)])

    def offsets(t, a, b):
        add("V", lambda: V.tensor_scalar(T["of%d" % t][:, a:b], T["ab%d" % t][:, a:b], T.pf[:, 1:2], None, ALU.add),
            [R("ab%d" % t, a, b), R("pf")], [R("of%d" % t, a, b)])

    def unit(b):
        quant("qe", "se", 128 * b, 128 * b + 128, T.band[:, 3 - b:515 - b], [R("band")])

    def size(t):
        return 1.0 if t == 0 else 0.015625

    def sign(t):
        cs = T["cs%d" % t]
        add("S", lambda: S.activation(cs[:, 0:1], T.ps[:, 512 * 5:512 * 5 + 1], ACT.Sign, bias=T.tiny[:, 0:1]),
            [bank(5), R("tiny")], [R("cs%d" % t, 0, 1)])
        add("S", lambda: S.activation(cs[:, 1:2], cs[:, 0:1], ACT.Copy, scale=0.5 * size(t)),
            [R("cs%d" % t, 0, 1)], [R("cs%d" % t, 1, 2)])

    def gather(t, q, name, a, b, first):
        cs, of, bt = T["cs%d" % t], T["of%d" % t], T["bt%d" % t]
        la, lb = first + a // 4, first + b // 4
        out = T[name][:, 4 * a:4 * b]
        if q == "S":
            add("S", lambda: S.activation(out, bt[:].indirect(of[:, la:lb]), ACT.Copy, scale=cs[:, 1:2]),
                [R("bt%d" % t), R("of%d" % t, la, lb), R("cs%d" % t, 1, 2)], [R(name, a, b)])
        else:
            add("V", lambda: V.tensor_scalar(out, bt[:].indirect(of[:, la:lb]), cs[:, 0:1], 0.5 * size(t),
                                             ALU.mult, ALU.mult),
                [R("bt%d" % t), R("of%d" % t, la, lb), R("cs%d" % t, 0, 1)], [R(name, a, b)])

    def send(t):
        dst = T.cores[(rank + STEP[t]) % n_ranks]
        rid, pid, _ = topo.addr(dst)
        m = topo.mask(core, dst)
        arr = T.sem["arr%d" % t]
        add("G", lambda: g.remote_dma(T["lq%d" % t][:].bitcast(dt.uint8), T["qg%d" % t][:].bitcast(dt.uint8),
                                      arr, T.sem.loc, pid, rid, m), [R("qg%d" % t)], [])
        add("G", lambda: g.remote_dma(T["ls%d" % t][:], T["sg%d" % t][:], arr, T.sem.loc, pid, rid, m),
            [R("sg%d" % t)], [])
        return 2 * len(topo.engines(core, dst))

    def subtract(t, a, b):
        name = "el%d" % t if b <= TL else "xs%d" % (t + 1)
        add("V", lambda: V.tensor_tensor(T[name][:, 4 * a:4 * b], T["xs%d" % t][:, 4 * a:4 * b],
                                         T["ge%d" % t][:, 4 * a:4 * b], ALU.subtract),
            [R("xs%d" % t, a, b), R("ge%d" % t, a, b)], [R(name, a, b)])

    def arrived(t, b):
        xn = T["xs%d" % (t + 1)]
        add("V", lambda: V.tensor_tensor(xn[:, b:4 * TL:4], T["el%d" % t][:, b:4 * TL:4],
                                         T.ps[:, 512 * b:512 * b + TL], ALU.subtract),
            [R("el%d" % t), bank(b)], [R("xs%d" % (t + 1), 0, TL, b)])

    def halve(t, a, e):
        add("S", lambda: S.activation(T["aux%d" % t][:, 4 * a:4 * e], T["bt%d" % t][:, 4 * a:4 * e], ACT.Copy,
                                      scale=32.0 * size(t)),
            [R("bt%d" % t, a, e)], [R("aux%d" % t, a, e)])

    def layer(t, b, late):
        a, e = (0, TL) if late else (TL, C)
        mm(b if late else EARLY_BANK[b], "wq", "wsc", 128 * b, "qx%d" % (t + 1), "sx%d" % (t + 1), a, e)

    def beam(t, b, late):
        a, e = (0, TL) if late else (TL, C)
        k = b if late else EARLY_BANK[b]
        add("V", lambda: V.tensor_tensor(T["bt%d" % (t + 1)][:, 4 * a + b:4 * e:4], T.ps[:, 512 * k:512 * k + e - a],
                                         T["aux%d" % t][:, 4 * a + b:4 * e:4], ALU.add),
            [bank(k), R("aux%d" % t, a, e)], [R("bt%d" % (t + 1), a, e, b)])

    def beam_col0(t, b):
        add("S", lambda: S.activation(T.z[:, b:b + 1], T.ps[:, 512 * b:512 * b + 1], ACT.Identity,
                                      bias=T.hcol[:, 4 * t + b:4 * t + b + 1], scale=0.015625),
            [bank(b), R("hcol", 4 * t, 4 * t + 4)], [R("z", b, b + 1)])

    add("Y", lambda: Y.dma_start(T.cc[:, 0:20], T.co[:]), [], [R("cc", 0, 20)], sem="lcc")
    add("Y", lambda: Y.dma_start(T.cc[:, 20:44], T.cn[:]), [], [R("cc", 20, 44)], sem="lcc")
    add("Y", lambda: Y.dma_start(T.us[:], T.u[:]), [], [R("us")], sem="lu")
    add("Y", lambda: Y.dma_start(T.xs0[:, 4 * HALF:4 * C], T.x[:, 4 * HALF:4 * C]), [], [R("xs0", HALF, C)], sem="lx1")
    add("Y", lambda: Y.dma_start(T.xs0[:, 0:4 * HALF], T.x[:, 0:4 * HALF]), [], [R("xs0", 0, HALF)], sem="lx0")
    add("Y", lambda: Y.dma_start(T.bt0[:, 0:4 * TL], T.bm[:, 0:4 * TL]), [], [R("bt0", 0, TL)], sem="lb0")
    add("Y", lambda: Y.dma_start(T.bt0[:, 4 * TL:4 * C], T.bm[:, 4 * TL:4 * C]), [], [R("bt0", TL, C)], sem="lb1")
    add("Y", lambda: Y.dma_start(T.wq[:].bitcast(dt.uint8), T.wc[:]), [], [R("wq")], sem="lw")
    add("Y", lambda: Y.dma_start(T.wsc[:], T.ws[:]), [], [R("wsc")], sem="lw")

    iota("pi", 0, 1, [[0, 1]], 1, whole=True)
    iota("lf", 8, 24, [[32, 2], [4, 4], [16, 2]], 0)
    iota("lf", 0, 8, [[16, 8]], 0)
    iota("lf", 24, 40, [[128, 2], [4, 8]], 0)
    iota("ramp", 0, C, [[1, C]], 0)
    iota("nil", 0, HALF, [[0, HALF]], 0)
    iota("row", 1, 3, [[1, 2]], 0)
    iota("z", 4, 512, [[0, 508]], 0)
    add("V", lambda: V.memset(T.band[:], 0.0), [], [R("band")])
    add("V", lambda: V.memset(T.c4[:, 44:64], 0.0), [], [R("c4", 44, 64)])
    add("V", lambda: V.memset(T.tiny[:], -TINY), [], [R("tiny")])
    add("V", lambda: V.tensor_scalar(T.pi[:, 1:2], T.pi[:, 0:1], 3, None, ALU.bitwise_and), [R("pi", 0, 1)], [R("pi", 1, 2)])
    add("V", lambda: V.tensor_scalar(T.pi[:, 2:3], T.pi[:, 0:1], 2, 3, ALU.logical_shift_right, ALU.bitwise_and),
        [R("pi", 0, 1)], [R("pi", 2, 3)])
    add("V", lambda: V.tensor_copy(T.pf[:, 0:3], T.pi[:, 0:3]), [R("pi", 0, 3)], [R("pf", 0, 3)])
    add("V", lambda: V.tensor_scalar(T.l16[:, 8:24], T.lf[:, 8:24], T.pf[:, 2:3], None, ALU.add),
        [R("lf", 8, 24), R("pf", 2, 3)], [R("l16", 8, 24)])
    add("V", lambda: V.tensor_scalar(T.pf[:, 3:4], T.pf[:, 1:2], 32.0, T.pf[:, 2:3], ALU.mult, ALU.add),
        [R("pf", 1, 3)], [R("pf", 3, 4)])
    add("V", lambda: V.tensor_copy(T.l16[:, 0:8], T.lf[:, 0:8]), [R("lf", 0, 8)], [R("l16", 0, 8)])
    add("V", lambda: V.tensor_scalar(T.l16[:, 24:40], T.lf[:, 24:40], T.pf[:, 3:4], None, ALU.add),
        [R("lf", 24, 40), R("pf", 3, 4)], [R("l16", 24, 40)])

    add("V", lambda: V.tensor_scalar(T.c4[:, 0:44], T.cc[:], 4.0, None, ALU.mult), [R("cc")], [R("c4", 0, 44)])
    add("V", lambda: V.tensor_copy(T.co16[:], T.cc[:, 0:20]), [R("cc")], [R("co16")])
    add("V", lambda: V.transpose(T.c4t[:], T.c4[:]), [R("c4")], [R("c4t")])
    add("S", lambda: S.activation(T.c4h[:], T.c4t[:].indirect(T.l16[:, 8:24]), ACT.Copy), [R("c4t"), R("l16", 8, 24)], [R("c4h")])
    quant("qu", "su", 0, 128, T.us[:], [R("us")])
    add("S", lambda: S.activation(T.sur[:], T.su[:].indirect(T.l16[:, 0:8]), ACT.Copy), [R("su"), R("l16", 0, 8)], [R("sur")])
    add("S", lambda: S.activation(T.coord[:], T.ramp[:].indirect(T.co16[:]), ACT.Copy), [R("ramp"), R("co16")], [R("coord")])
    add("V", lambda: V.tensor_copy(T.qur[:].bitcast(dt.uint32), T.qu[:].bitcast(dt.uint32).indirect(T.l16[:, 0:8])),
        [R("qu"), R("l16", 0, 8)], [R("qur")])
    quant_x(0, HALF, C)
    mm(4, "qur", "sur", 0, "qx0", "sx0", HALF, C)
    add("V", lambda: V.transpose(T.c4u[:], T.c4h[:]), [R("c4h")], [R("c4u")])
    quant_x(0, 0, HALF)
    mm(6, "qur", "sur", 0, "qx0", "sx0", 0, HALF)
    scan(0, 1, 4)
    add("S", lambda: S.activation(T.tab[:], T.c4u[:].indirect(T.l16[:, 24:35]), ACT.Copy), [R("c4u"), R("l16", 24, 40)], [R("tab")])
    count(0, 1)
    scan(0, 0, 6)
    count(0, 0)
    peak1(0)
    higher(0)
    quant("qz0", "sz0", 0, 128, T.bt0[:, 0:4 * TL], [R("bt0", 0, TL)])
    mm(5, "qur", "sur", 0, "qz0", "sz0", 0, 128)
    add("V", lambda: V.tensor_scalar(T.band[:, 3:515:4], T.ramp[:, 0:128], T.pf[:, 0:1], None, ALU.is_equal),
        [R("ramp"), R("pf", 0, 1)], [R("band")])
    unit(0)
    peaks16(0)
    sign(0)
    peak_coords(0)
    unit(1)
    unit(2)
    for e in range(3):
        dist(0, e)
    offsets(0, 0, NT)

    sent = 0
    for t in range(ROUNDS):
        last = t == ROUNDS - 1
        qn, sn = "qx%d" % (t + 1), "sx%d" % (t + 1)
        store_peaks(t)
        gather(t, "V", "gt%d" % t, 0, CUT, 0)
        gather(t, "S", "gt%d" % t, CUT, TL, 0)
        if t == 0:
            offsets(0, NT, NT + NO)
        quant("qg%d" % t, "sg%d" % t, 0, TL, T["gt%d" % t][:], [R("gt%d" % t)])
        sent += send(t)
        src = T.cores[(rank - STEP[t]) % n_ranks]
        landed = 2 * len(topo.engines(src, core))
        own, cut = OWN[t]
        for a, b in [(own, cut)] + EARLY + [(cut, TL)]:
            gather(t, "S", "ge%d" % t, a, b, NT)
        if last:
            quant("qv", "sv", 0, 128, T.vs[:], [R("vs")])
        gather(t, "V", "ge%d" % t, 0, own, NT)
        for a, b in [(0, cut)] + EARLY + [(cut, TL)]:
            subtract(t, a, b)
        quant_x(t + 1, TL, C)
        if t == 0:
            unit(3)
        if not last:
            halve(t, TL, C)
            col0 = T.bt0 if t == 0 else T.z
            add("S", lambda t=t, col0=col0: S.activation(T.hcol[:, 4 * t:4 * t + 4], col0[:, 0:4], ACT.Copy, scale=0.5),
                [R("z", 0, 4), R("bt0")], [R("hcol", 4 * t, 4 * t + 4)])
            halve(t, 0, TL)
        for b in range(4):
            mm(b, "qe", "se", 128 * b, "lq%d" % t, "ls%d" % t, 0, TL, ext=[("arr%d" % t, landed)] if b == 0 else [])
        if last:
            add("Y", lambda: Y.dma_start(T.oc[:, 4 * TL:4 * C], T[qn][:, TL:C].bitcast(dt.uint8)), [R(qn, TL, C)], [], sem="sty")
            mm(4, "qv", "sv", 0, qn, sn, TL, C)
            add("S", lambda: S.activation(T.ysb[:, TL:C], T.ps[:, 512 * 4:512 * 4 + C - TL], ACT.Copy),
                [bank(4)], [R("ysb", TL, C)])
            add("Y", lambda: Y.dma_start(T.y[:, TL:C], T.ysb[:, TL:C]), [R("ysb", TL, C)], [], sem="sty")
        else:
            mm(4, "qur", "sur", 0, qn, sn, HALF, C)
            layer(t, 0, False)
            layer(t, 1, False)
        for b in range(4):
            arrived(t, b)
        quant_x(t + 1, 0, TL)
        if last:
            break
        if t == 0:
            add("Y", lambda: Y.dma_start(T.vs[:], T.v[:]), [R("xs1", 0, TL, 0)], [R("vs")], sem="lv")
        mm(7, "qur", "sur", 0, qn, sn, 0, HALF)
        for b in range(4):
            layer(t, b, True)
        scan(t + 1, 1, 4)
        count(t + 1, 1)
        peak1(t + 1)
        beam(t, 0, False)
        layer(t, 2, False)
        scan(t + 1, 0, 7)
        layer(t, 3, False)
        beam_col0(t, 0)
        beam_col0(t, 1)
        count(t + 1, 0)
        higher(t + 1)
        beam(t, 1, False)
        beam(t, 0, True)
        beam(t, 1, True)
        beam_col0(t, 2)
        beam_col0(t, 3)
        peaks16(t + 1)
        beam(t, 2, True)
        quant("qz%d" % (t + 1), "sz%d" % (t + 1), 0, 128, T.z[:], [R("z")])
        mm(5, "qur", "sur", 0, "qz%d" % (t + 1), "sz%d" % (t + 1), 0, 128)
        peak_coords(t + 1)
        beam(t, 3, True)
        beam(t, 2, False)
        for e in range(3):
            dist(t + 1, e)
        sign(t + 1)
        offsets(t + 1, 0, NT)
        beam(t, 3, False)
        offsets(t + 1, NT, NT + NO)

    qn, sn = "qx%d" % ROUNDS, "sx%d" % ROUNDS
    mm(5, "qv", "sv", 0, qn, sn, 0, TL)
    add("Y", lambda: Y.dma_start(T.oc[:, 0:4 * TL], T[qn][:, 0:TL].bitcast(dt.uint8)), [R(qn, 0, TL)], [], sem="sty")
    for k in range(4):
        q, e, sem = ("Y", Y, "sty") if k == 0 else ("S", S, "sts")
        add(q, lambda k=k, e=e: e.dma_start(T.osc[4 * k:4 * k + 4, :], T[sn][32 * k:32 * k + 4, :]), [R(sn)], [], sem=sem)
    add("V", lambda: V.tensor_copy(T.ysb[:, 0:TL], T.ps[:, 512 * 5:512 * 5 + TL]), [bank(5)], [R("ysb", 0, TL)])
    add("Y", lambda: Y.dma_start(T.y[:, 0:TL], T.ysb[:, 0:TL]), [R("ysb", 0, TL)], [], sem="sty")

    emit(g, T, ops, [("G", "loc", sent), ("Y", "sty", None), ("S", "sts", None)])
